import numpy as np
import ml_dtypes


def mxq(x, axis, fmt="e4m3"):
    dtype, down = {"e4m3": (ml_dtypes.float8_e4m3fn, 7), "e5m2": (ml_dtypes.float8_e5m2, 14)}[fmt]
    v = np.moveaxis(np.asarray(x, np.float32).astype(ml_dtypes.bfloat16).astype(np.float64), axis, -1)
    blocks = v.reshape(v.shape[:-1] + (-1, 32))
    amax = np.abs(blocks).max(-1, keepdims=True)
    byte = np.maximum(np.where(amax > 0, np.frexp(amax)[1] - 1 + 127, 0) - down, 1)
    scale = np.exp2(byte - 127.0)
    codes = (blocks / scale).astype(np.float32).astype(dtype).astype(np.float64)
    return np.moveaxis((codes * scale).reshape(v.shape), -1, axis)


WIDE = False


def mx_kscale(k):
    if not WIDE:
        return np.ones(k)
    levels = np.array([10, -10, 5, -5, 0])
    if k % 512:
        return np.exp2(np.random.permutation(np.resize(levels, k // 32))).repeat(32)
    a = np.empty((k // 512, 16))
    for p in range(k // 512):
        a[p, :8] = np.random.permutation(np.resize(levels, 8))
        for g in range(8):
            far = levels[np.abs(levels - a[p, g]) >= 10]
            a[p, g + 8] = far[np.random.randint(len(far))]
    return np.exp2(a.ravel()).repeat(32)


def f64(x):
    return np.asarray(x).astype(np.float64)


def striped(idx):
    return np.tile(idx.reshape(-1, 16).T, (8, 1)).astype(np.uint16)


def unstriped(offs):
    return offs[:16].T.reshape(-1).astype(np.int64)


def pack_weight(w):
    k, n = w.shape
    w = f64(np.asarray(w, np.float32).astype(ml_dtypes.bfloat16)).reshape(k // 32, 32, n)
    amax = np.abs(w).max(1)
    byte = np.clip(np.where(amax > 0, np.frexp(amax)[1] - 1 + 127 - 7, 1), 1, 254)
    scaled = (w * np.exp2(127.0 - byte)[:, None, :]).reshape(k, n).astype(np.float32)
    words = np.ascontiguousarray(scaled.reshape(k // 512, 128, 4, n).transpose(0, 1, 3, 2)).astype(ml_dtypes.float8_e4m3fn).view(np.uint8)
    return words, np.ascontiguousarray(byte.astype(np.uint8).reshape(k // 512, 16, n))


def unpack_weight(words, scales):
    g, p, n, _ = words.shape
    vals = np.ascontiguousarray(words).view(ml_dtypes.float8_e4m3fn).astype(np.float64) * np.repeat(np.exp2(scales.astype(np.float64) - 127.0), 8, axis=1)[..., None]
    return vals.transpose(0, 1, 3, 2).reshape(g * 512, n)


def gelu(v):
    return 0.5 * v * (1.0 + np.tanh(np.sqrt(2.0 / np.pi) * (v + 0.044715 * v**3)))


K, T, S, V, H, N = 512, 4096, 1536, 768, 512, 128


def setup_inputs():
    n = np.random.standard_normal
    s = mx_kscale(K)[:, None]
    u = mx_kscale(H)
    packed_xT = pack_weight(n((K, T)) * s)
    return {
        "x_words": packed_xT[0],
        "x_scales": packed_xT[1],
        "w1": (n((K, H)) / np.sqrt(K) / s * u).astype(np.float32),
        "w2": (n((H, N)) / np.sqrt(2 * H) / u[:, None]).astype(np.float32),
        "w3": (n((H, N)) / np.sqrt(2 * H) / u[:, None]).astype(np.float32),
        "offs": striped(np.random.permutation(T)[:S]),
    }


def reference(x_words, x_scales, w1, w2, w3, offs):
    xq = unpack_weight(x_words, x_scales)[:, unstriped(offs)]
    h = gelu(mxq(f64(w1), 0, "e4m3").T @ xq)
    low = 0.5 * (h[:, :V] + h[:, V:2 * V])
    high = 0.5 * (h[:, :V] - h[:, V:2 * V])
    return mxq(f64(w2), 0, "e4m3").T @ mxq(low, 0, "e4m3") + mxq(f64(w3), 0, "e4m3").T @ mxq(high, 0, "e4m3")

@@ -1,0 +1,181 @@
+from contextlib import ExitStack
+
+import concourse.mybir as mybir
+
+K, T, S, V, H, N = 512, 4096, 1536, 768, 512, 128
+FLOPS = 2 * K * H * S + 2 * 2 * H * N * V
+
+F32 = mybir.dt.float32
+BF16 = mybir.dt.bfloat16
+I32 = mybir.dt.int32
+U32 = mybir.dt.uint32
+U16 = mybir.dt.uint16
+U8 = mybir.dt.uint8
+FP8X4 = mybir.dt.float8_e4m3fn_x4
+GELU = mybir.ActivationFunctionType.Gelu_apprx_tanh
+COPY = mybir.ActivationFunctionType.Copy
+ADD = mybir.AluOpType.add
+SUBTRACT = mybir.AluOpType.subtract
+
+P = 128
+PACK = 4
+GROUP = 128
+GROUPS = S // GROUP
+PAIR_GROUPS = V // GROUP
+SLICE = 512
+X_HEAD = 1024
+W1_PARTS = 4
+CHUNKS = ((0, 1), (1, 3), (3, 5), (5, 6))
+
+
+def tile_picked_haar_gelu_p_kernel(tc, x_words, x_scales, w1, w2, w3, offs, out):
+    nc = tc.nc
+    with ExitStack() as ctx:
+        lists = ctx.enter_context(tc.tile_pool(name="lists", bufs=1))
+        keep = ctx.enter_context(tc.tile_pool(name="keep", bufs=1))
+        hidden_psum = ctx.enter_context(tc.psum_pool(name="hidden_psum", bufs=6))
+        out_psum = ctx.enter_context(tc.psum_pool(name="out_psum", bufs=2))
+
+        offsets = lists.tile([P, S // 16], U16, name="offsets")
+        nc.sync.dma_start(offsets[:], offs)
+
+        warm = keep.tile([P, 2], F32, name="warm")
+        nc.vector.memset(warm[:, 0:1], 0.0)
+        nc.scalar.activation(warm[:, 1:2], warm[:, 0:1], GELU)
+
+        word_table = keep.tile([P, T], U32, name="word_table", align_bytes=64)
+        scale_table = keep.tile([P, T], U8, name="scale_table", align_bytes=64)
+        words_hbm = x_words[0].rearrange("p n t -> p (n t)").bitcast(I32)
+        scales_hbm = x_scales[0].bitcast(I32)
+        nc.vector.memset(scale_table[:].bitcast(I32), 0)
+        nc.sync.dma_start(word_table[:, :X_HEAD].bitcast(I32), words_hbm[:, :X_HEAD])
+        for q in range(4):
+            nc.sync.dma_start(scale_table[32 * q : 32 * q + 4, :].bitcast(I32), scales_hbm[4 * q : 4 * q + 4, :])
+        nc.sync.dma_start(word_table[:, X_HEAD:].bitcast(I32), words_hbm[:, X_HEAD:])
+
+        part = H // W1_PARTS
+        w1_rows = w1.rearrange("(p j) c -> p j c", j=PACK)
+        w1_raw = []
+        for a in range(W1_PARTS):
+            raw = keep.tile([P, PACK, part], F32, name=f"w1_raw{a}")
+            nc.sync.dma_start(raw[:], w1_rows[:, :, a * part : (a + 1) * part])
+            w1_raw.append(raw)
+        band_raw = []
+        for b, w in enumerate((w2, w3)):
+            raw = keep.tile([P, PACK, N], F32, name=f"band_raw{b}")
+            nc.sync.dma_start(raw[:], w.rearrange("(p j) m -> p j m", j=PACK))
+            band_raw.append(raw)
+
+        picked_scales = []
+        for s in range(S // SLICE):
+            picked = keep.tile([P, SLICE], U8, name=f"picked_scales{s}", align_bytes=64)
+            nc.vector.tensor_copy(picked[:], scale_table[:].indirect(offsets[:, s * SLICE // 16 : (s + 1) * SLICE // 16]))
+            picked_scales.append(picked)
+        picked_words = {}
+
+        def gather_words(s):
+            tag = "staging" if s == 2 else f"picked_words{s}"
+            picked_words[s] = keep.tile([P, SLICE], U32, name=f"picked_words{s}", tag=tag, align_bytes=64)
+            nc.vector.tensor_copy(
+                picked_words[s][:], word_table[:].indirect(offsets[:, s * SLICE // 16 : (s + 1) * SLICE // 16])
+            )
+
+        gather_words(0)
+        gather_words(1)
+
+        w1_bf16 = keep.tile([P, PACK, P, PACK], BF16, name="w1_bf16", tag="staging", align_bytes=64)
+        w1_codes = keep.tile([P, H], U32, name="w1_codes", align_bytes=64)
+        w1_scales = keep.tile([P, H], U8, name="w1_scales", align_bytes=64)
+        part_m = P // W1_PARTS
+        for a in range(W1_PARTS):
+            nc.scalar.copy(
+                w1_bf16[:, :, a * part_m : (a + 1) * part_m, :].rearrange("p t m j -> p m t j"),
+                w1_raw[a][:].rearrange("p j (m t) -> p m t j", t=PACK),
+            )
+        for t in range(PACK):
+            nc.vector.quantize_mx(
+                out=w1_codes[:, t * P : (t + 1) * P].bitcast(FP8X4),
+                scales=w1_scales[:, t * P : (t + 1) * P],
+                in_=w1_bf16[:, t, :, :].rearrange("p m j -> p (m j)"),
+            )
+        gather_words(2)
+
+        hidden = keep.tile([P, GROUPS, GROUP * PACK], F32, name="hidden")
+
+        def first_layer(g):
+            s, first = divmod(g * GROUP, SLICE)
+            cols = slice(first, first + GROUP)
+            bank = hidden_psum.tile([P, PACK, GROUP], F32, name="hidden_bank")
+            for t in range(PACK):
+                nc.tensor.matmul_mx(
+                    out=bank[:, t, :],
+                    lhsT=w1_codes[:, t * P : (t + 1) * P].bitcast(FP8X4),
+                    lhsT_scale=w1_scales[:, t * P : (t + 1) * P],
+                    rhs=picked_words[s][:, cols].bitcast(FP8X4),
+                    rhs_scale=picked_scales[s][:, cols],
+                    start=True,
+                    stop=True,
+                )
+            nc.scalar.activation(
+                hidden[:, g, :].rearrange("p (n t) -> p n t", t=PACK), bank[:].rearrange("p t n -> p n t"), GELU
+            )
+
+        band_bf16 = keep.tile([P, 2, N, PACK], BF16, name="band_bf16", align_bytes=64)
+        band_codes = keep.tile([P, 2 * N], U32, name="band_codes", align_bytes=64)
+        band_scales = keep.tile([P, 2 * N], U8, name="band_scales", align_bytes=64)
+
+        def band_weights():
+            for b in range(2):
+                nc.scalar.copy(
+                    band_bf16[:, b, :, :].rearrange("p (c i) j -> p c j i", i=PACK),
+                    band_raw[b][:].rearrange("p j (c i) -> p c j i", i=PACK),
+                )
+            nc.vector.quantize_mx(
+                out=band_codes[:].bitcast(FP8X4), scales=band_scales[:], in_=band_bf16[:].rearrange("p b m j -> p (b m j)")
+            )
+
+        bands = {}
+
+        def haar(c):
+            lo, hi = CHUNKS[c]
+            width = (hi - lo) * GROUP
+            pair = keep.tile([P, 2, width * PACK], BF16, name=f"bands{c}", align_bytes=64)
+            first = hidden[:, lo:hi, :].rearrange("p g n -> p (g n)")
+            second = hidden[:, PAIR_GROUPS + lo : PAIR_GROUPS + hi, :].rearrange("p g n -> p (g n)")
+            nc.vector.tensor_tensor(pair[:, 0, :], first, second, ADD)
+            nc.vector.tensor_tensor(pair[:, 1, :], first, second, SUBTRACT)
+            bands[c] = pair
+
+        def second_layer(c):
+            lo, hi = CHUNKS[c]
+            width = (hi - lo) * GROUP
+            codes = keep.tile([P, 2, width], U32, name=f"codes{c}", align_bytes=64)
+            scales = keep.tile([P, 2, width], U8, name=f"scales{c}", align_bytes=64)
+            bank = out_psum.tile([P, width], F32, name="out_bank")
+            for b in range(2):
+                nc.vector.quantize_mx(out=codes[:, b, :].bitcast(FP8X4), scales=scales[:, b, :], in_=bands[c][:, b, :])
+            for b in range(2):
+                nc.tensor.matmul_mx(
+                    out=bank[:],
+                    lhsT=band_codes[:, b * N : (b + 1) * N].bitcast(FP8X4),
+                    lhsT_scale=band_scales[:, b * N : (b + 1) * N],
+                    rhs=codes[:, b, :].bitcast(FP8X4),
+                    rhs_scale=scales[:, b, :],
+                    start=(b == 0),
+                    stop=(b == 1),
+                )
+            result = keep.tile([P, width], F32, name=f"result{c}")
+            nc.scalar.activation(result[:], bank[:], COPY, scale=0.5)
+            nc.sync.dma_start(out[:, lo * GROUP : hi * GROUP], result[:])
+
+        for c, (lo, hi) in enumerate(CHUNKS):
+            for g in range(lo, hi):
+                first_layer(g)
+                first_layer(PAIR_GROUPS + g)
+            if c == 1:
+                band_weights()
+            haar(c)
+            if c == 1:
+                second_layer(0)
+            if c >= 1:
+                second_layer(c)

@@ -23,8 +23,6 @@ GROUP = 128
 GROUPS = S // GROUP
 PAIR_GROUPS = V // GROUP
 SLICE = 512
-X_HEAD = 1024
-W1_PARTS = 4
 CHUNKS = ((0, 1), (1, 3), (3, 5), (5, 6))
 
 
@@ -33,86 +31,64 @@ def tile_picked_haar_gelu_p_kernel(tc, x_words, x_scales, w1, w2, w3, offs, out)
     with ExitStack() as ctx:
         lists = ctx.enter_context(tc.tile_pool(name="lists", bufs=1))
         keep = ctx.enter_context(tc.tile_pool(name="keep", bufs=1))
-        hidden_psum = ctx.enter_context(tc.psum_pool(name="hidden_psum", bufs=6))
-        out_psum = ctx.enter_context(tc.psum_pool(name="out_psum", bufs=2))
+        hidden_psum = ctx.enter_context(tc.psum_pool(name="hidden_psum", bufs=5))
+        out_psum = ctx.enter_context(tc.psum_pool(name="out_psum", bufs=3))
 
         offsets = lists.tile([P, S // 16], U16, name="offsets")
+        scale_table = keep.tile([P, T], U8, name="scale_table", align_bytes=64)
+        word_table = keep.tile([P, T], U32, name="word_table", align_bytes=64)
+        w1_raw = keep.tile([P, PACK, H], F32, name="w1_raw", tag="raw_weights")
+        nc.sync.dma_start(scale_table[16:32, :].bitcast(I32), x_scales[0].bitcast(I32))
         nc.sync.dma_start(offsets[:], offs)
+        nc.sync.dma_start(w1_raw[:], w1.rearrange("(p j) c -> p j c", j=PACK))
+        nc.sync.dma_start(word_table[:].bitcast(I32), x_words[0].rearrange("p n t -> p (n t)").bitcast(I32))
 
         warm = keep.tile([P, 2], F32, name="warm")
         nc.vector.memset(warm[:, 0:1], 0.0)
         nc.scalar.activation(warm[:, 1:2], warm[:, 0:1], GELU)
 
-        word_table = keep.tile([P, T], U32, name="word_table", align_bytes=64)
-        scale_table = keep.tile([P, T], U8, name="scale_table", align_bytes=64)
-        words_hbm = x_words[0].rearrange("p n t -> p (n t)").bitcast(I32)
-        scales_hbm = x_scales[0].bitcast(I32)
-        nc.vector.memset(scale_table[:].bitcast(I32), 0)
-        nc.sync.dma_start(word_table[:, :X_HEAD].bitcast(I32), words_hbm[:, :X_HEAD])
-        for q in range(4):
-            nc.sync.dma_start(scale_table[32 * q : 32 * q + 4, :].bitcast(I32), scales_hbm[4 * q : 4 * q + 4, :])
-        nc.sync.dma_start(word_table[:, X_HEAD:].bitcast(I32), words_hbm[:, X_HEAD:])
+        for first, last in ((0, 16), (32, 64), (64, P)):
+            nc.vector.memset(scale_table[first:last, :].bitcast(I32), 0)
+        picked_rows = keep.tile([P, S], U8, name="picked_rows", align_bytes=64)
+        picked_scales = keep.tile([P, S], U8, name="picked_scales", align_bytes=64)
+        nc.vector.memset(picked_scales[:].bitcast(I32), 0)
+        nc.vector.tensor_copy(picked_rows[:], scale_table[:].indirect(offsets[:]))
+        for r in range(4):
+            nc.sync.dma_start(picked_scales[r:P:32, :].bitcast(I32), picked_rows[16 + r : 32 : 4, :].bitcast(I32))
 
-        part = H // W1_PARTS
-        w1_rows = w1.rearrange("(p j) c -> p j c", j=PACK)
-        w1_raw = []
-        for a in range(W1_PARTS):
-            raw = keep.tile([P, PACK, part], F32, name=f"w1_raw{a}")
-            nc.sync.dma_start(raw[:], w1_rows[:, :, a * part : (a + 1) * part])
-            w1_raw.append(raw)
-        band_raw = []
-        for b, w in enumerate((w2, w3)):
-            raw = keep.tile([P, PACK, N], F32, name=f"band_raw{b}")
-            nc.sync.dma_start(raw[:], w.rearrange("(p j) m -> p j m", j=PACK))
-            band_raw.append(raw)
-
-        picked_scales = []
-        for s in range(S // SLICE):
-            picked = keep.tile([P, SLICE], U8, name=f"picked_scales{s}", align_bytes=64)
-            nc.vector.tensor_copy(picked[:], scale_table[:].indirect(offsets[:, s * SLICE // 16 : (s + 1) * SLICE // 16]))
-            picked_scales.append(picked)
-        picked_words = {}
-
-        def gather_words(s):
-            tag = "staging" if s == 2 else f"picked_words{s}"
-            picked_words[s] = keep.tile([P, SLICE], U32, name=f"picked_words{s}", tag=tag, align_bytes=64)
-            nc.vector.tensor_copy(
-                picked_words[s][:], word_table[:].indirect(offsets[:, s * SLICE // 16 : (s + 1) * SLICE // 16])
-            )
-
-        gather_words(0)
-        gather_words(1)
-
-        w1_bf16 = keep.tile([P, PACK, P, PACK], BF16, name="w1_bf16", tag="staging", align_bytes=64)
+        w1_bf16 = keep.tile([P, PACK, P, PACK], BF16, name="w1_bf16", align_bytes=64)
         w1_codes = keep.tile([P, H], U32, name="w1_codes", align_bytes=64)
         w1_scales = keep.tile([P, H], U8, name="w1_scales", align_bytes=64)
-        part_m = P // W1_PARTS
-        for a in range(W1_PARTS):
-            nc.scalar.copy(
-                w1_bf16[:, :, a * part_m : (a + 1) * part_m, :].rearrange("p t m j -> p m t j"),
-                w1_raw[a][:].rearrange("p j (m t) -> p m t j", t=PACK),
-            )
-        for t in range(PACK):
-            nc.vector.quantize_mx(
-                out=w1_codes[:, t * P : (t + 1) * P].bitcast(FP8X4),
-                scales=w1_scales[:, t * P : (t + 1) * P],
-                in_=w1_bf16[:, t, :, :].rearrange("p m j -> p (m j)"),
-            )
-        gather_words(2)
+        dealt = w1_bf16[:].rearrange("p t m j -> p m t j")
+        rows = w1_raw[:].rearrange("p j (m t) -> p m t j", t=PACK)
+        nc.scalar.copy(dealt[:, : P // 2], rows[:, : P // 2])
+        nc.vector.tensor_copy(dealt[:, P // 2 :], rows[:, P // 2 :])
+        nc.vector.quantize_mx(
+            out=w1_codes[:].bitcast(FP8X4), scales=w1_scales[:], in_=w1_bf16[:].rearrange("p t m j -> p (t m j)")
+        )
+
+        band_raw = keep.tile([P, 2, PACK, N], F32, name="band_raw", tag="raw_weights")
+        for b, w in enumerate((w2, w3)):
+            nc.sync.dma_start(band_raw[:, b], w.rearrange("(p j) m -> p j m", j=PACK))
+
+        picked_words = []
+        for s in range(S // SLICE):
+            picked = keep.tile([P, SLICE], U32, name=f"picked_words{s}", align_bytes=64)
+            nc.vector.tensor_copy(picked[:], word_table[:].indirect(offsets[:, s * SLICE // 16 : (s + 1) * SLICE // 16]))
+            picked_words.append(picked)
 
         hidden = keep.tile([P, GROUPS, GROUP * PACK], F32, name="hidden")
 
         def first_layer(g):
             s, first = divmod(g * GROUP, SLICE)
-            cols = slice(first, first + GROUP)
             bank = hidden_psum.tile([P, PACK, GROUP], F32, name="hidden_bank")
             for t in range(PACK):
                 nc.tensor.matmul_mx(
                     out=bank[:, t, :],
                     lhsT=w1_codes[:, t * P : (t + 1) * P].bitcast(FP8X4),
                     lhsT_scale=w1_scales[:, t * P : (t + 1) * P],
-                    rhs=picked_words[s][:, cols].bitcast(FP8X4),
-                    rhs_scale=picked_scales[s][:, cols],
+                    rhs=picked_words[s][:, first : first + GROUP].bitcast(FP8X4),
+                    rhs_scale=picked_scales[:, g * GROUP : (g + 1) * GROUP],
                     start=True,
                     stop=True,
                 )
@@ -124,36 +100,46 @@ def tile_picked_haar_gelu_p_kernel(tc, x_words, x_scales, w1, w2, w3, offs, out)
         band_codes = keep.tile([P, 2 * N], U32, name="band_codes", align_bytes=64)
         band_scales = keep.tile([P, 2 * N], U8, name="band_scales", align_bytes=64)
 
-        def band_weights():
+        def round_band_weights():
             for b in range(2):
                 nc.scalar.copy(
-                    band_bf16[:, b, :, :].rearrange("p (c i) j -> p c j i", i=PACK),
-                    band_raw[b][:].rearrange("p j (c i) -> p c j i", i=PACK),
+                    band_bf16[:, b].rearrange("p (c i) j -> p c j i", i=PACK),
+                    band_raw[:, b].rearrange("p j (c i) -> p c j i", i=PACK),
                 )
+
+        def quantize_band_weights():
             nc.vector.quantize_mx(
                 out=band_codes[:].bitcast(FP8X4), scales=band_scales[:], in_=band_bf16[:].rearrange("p b m j -> p (b m j)")
             )
 
-        bands = {}
+        halves = {}
+        quantized = {}
 
         def haar(c):
             lo, hi = CHUNKS[c]
             width = (hi - lo) * GROUP
-            pair = keep.tile([P, 2, width * PACK], BF16, name=f"bands{c}", align_bytes=64)
+            bands = keep.tile([P, 2, width * PACK], BF16, name=f"bands{c}", align_bytes=64)
             first = hidden[:, lo:hi, :].rearrange("p g n -> p (g n)")
             second = hidden[:, PAIR_GROUPS + lo : PAIR_GROUPS + hi, :].rearrange("p g n -> p (g n)")
-            nc.vector.tensor_tensor(pair[:, 0, :], first, second, ADD)
-            nc.vector.tensor_tensor(pair[:, 1, :], first, second, SUBTRACT)
-            bands[c] = pair
+            nc.vector.tensor_tensor(bands[:, 0, :], first, second, ADD)
+            nc.vector.tensor_tensor(bands[:, 1, :], first, second, SUBTRACT)
+            halves[c] = bands
+
+        def quantize_bands(c):
+            lo, hi = CHUNKS[c]
+            width = (hi - lo) * GROUP
+            bands = halves[c]
+            codes = keep.tile([P, 2, width], U32, name=f"codes{c}", align_bytes=64)
+            scales = keep.tile([P, 2, width], U8, name=f"scales{c}", align_bytes=64)
+            for b in range(2):
+                nc.vector.quantize_mx(out=codes[:, b, :].bitcast(FP8X4), scales=scales[:, b, :], in_=bands[:, b, :])
+            quantized[c] = (codes, scales)
 
         def second_layer(c):
             lo, hi = CHUNKS[c]
             width = (hi - lo) * GROUP
-            codes = keep.tile([P, 2, width], U32, name=f"codes{c}", align_bytes=64)
-            scales = keep.tile([P, 2, width], U8, name=f"scales{c}", align_bytes=64)
+            codes, scales = quantized[c]
             bank = out_psum.tile([P, width], F32, name="out_bank")
-            for b in range(2):
-                nc.vector.quantize_mx(out=codes[:, b, :].bitcast(FP8X4), scales=scales[:, b, :], in_=bands[c][:, b, :])
             for b in range(2):
                 nc.tensor.matmul_mx(
                     out=bank[:],
@@ -168,14 +154,17 @@ def tile_picked_haar_gelu_p_kernel(tc, x_words, x_scales, w1, w2, w3, offs, out)
             nc.scalar.activation(result[:], bank[:], COPY, scale=0.5)
             nc.sync.dma_start(out[:, lo * GROUP : hi * GROUP], result[:])
 
+        last = len(CHUNKS) - 1
         for c, (lo, hi) in enumerate(CHUNKS):
+            if c == last:
+                round_band_weights()
             for g in range(lo, hi):
                 first_layer(g)
                 first_layer(PAIR_GROUPS + g)
-            if c == 1:
-                band_weights()
+        for c in range(len(CHUNKS)):
             haar(c)
-            if c == 1:
-                second_layer(0)
-            if c >= 1:
-                second_layer(c)
+            if c == last - 1:
+                quantize_band_weights()
+            quantize_bands(c)
+        for c in range(len(CHUNKS)):
+            second_layer(c)

@@ -1,6 +1,7 @@
 from contextlib import ExitStack
 
 import concourse.mybir as mybir
+from concourse.masks import make_identity
 
 K, T, S, V, H, N = 512, 4096, 1536, 768, 512, 128
 FLOPS = 2 * K * H * S + 2 * 2 * H * N * V
@@ -61,8 +62,8 @@ def tile_picked_haar_gelu_p_kernel(tc, x_words, x_scales, w1, w2, w3, offs, out)
         w1_scales = keep.tile([P, H], U8, name="w1_scales", align_bytes=64)
         dealt = w1_bf16[:].rearrange("p t m j -> p m t j")
         rows = w1_raw[:].rearrange("p j (m t) -> p m t j", t=PACK)
-        nc.scalar.copy(dealt[:, : P // 2], rows[:, : P // 2])
-        nc.vector.tensor_copy(dealt[:, P // 2 :], rows[:, P // 2 :])
+        nc.scalar.copy(dealt[:, :96], rows[:, :96])
+        nc.vector.tensor_copy(dealt[:, 96:], rows[:, 96:])
         nc.vector.quantize_mx(
             out=w1_codes[:].bitcast(FP8X4), scales=w1_scales[:], in_=w1_bf16[:].rearrange("p t m j -> p (t m j)")
         )
@@ -77,6 +78,7 @@ def tile_picked_haar_gelu_p_kernel(tc, x_words, x_scales, w1, w2, w3, offs, out)
             nc.vector.tensor_copy(picked[:], word_table[:].indirect(offsets[:, s * SLICE // 16 : (s + 1) * SLICE // 16]))
             picked_words.append(picked)
 
+        halves = {}
         hidden = keep.tile([P, GROUPS, GROUP * PACK], F32, name="hidden")
 
         def first_layer(g):
@@ -96,6 +98,38 @@ def tile_picked_haar_gelu_p_kernel(tc, x_words, x_scales, w1, w2, w3, offs, out)
                 hidden[:, g, :].rearrange("p (n t) -> p n t", t=PACK), bank[:].rearrange("p t n -> p n t"), GELU
             )
 
+        identity = keep.tile([P, P], F32, name="identity")
+        make_identity(nc, identity[:])
+
+        def first_layer_by_rows(g):
+            s, first = divmod(g * GROUP, SLICE)
+            bank = hidden_psum.tile([P, H], F32, name="hidden_bank")
+            nc.tensor.matmul_mx(
+                out=bank[:],
+                lhsT=picked_words[s][:, first : first + GROUP].bitcast(FP8X4),
+                lhsT_scale=picked_scales[:, g * GROUP : (g + 1) * GROUP],
+                rhs=w1_codes[:].bitcast(FP8X4),
+                rhs_scale=w1_scales[:],
+                start=True,
+                stop=True,
+            )
+            nc.scalar.activation(hidden[:, g, :], bank[:], GELU)
+
+        def haar_by_transposes(c):
+            g = CHUNKS[c][0]
+            negated = keep.tile([P, H], F32, name="negated")
+            nc.scalar.activation(negated[:], hidden[:, PAIR_GROUPS + g, :], COPY, scale=-1.0)
+            round_band_weights()
+            bands = keep.tile([P, 2, H], BF16, name=f"bands{c}", align_bytes=64)
+            for b, second in enumerate((hidden[:, PAIR_GROUPS + g, :], negated[:])):
+                bank = hidden_psum.tile([P, PACK, GROUP], F32, name="hidden_bank")
+                for t in range(PACK):
+                    cols = slice(t * P, (t + 1) * P)
+                    nc.tensor.matmul(bank[:, t, :], hidden[:, g, cols], identity[:], start=True, stop=False, is_transpose=True)
+                    nc.tensor.matmul(bank[:, t, :], second[:, cols], identity[:], start=False, stop=True, is_transpose=True)
+                nc.scalar.copy(bands[:, b, :].rearrange("p (n t) -> p n t", t=PACK), bank[:].rearrange("p t n -> p n t"))
+            halves[c] = bands
+
         band_bf16 = keep.tile([P, 2, N, PACK], BF16, name="band_bf16", align_bytes=64)
         band_codes = keep.tile([P, 2 * N], U32, name="band_codes", align_bytes=64)
         band_scales = keep.tile([P, 2 * N], U8, name="band_scales", align_bytes=64)
@@ -112,7 +146,6 @@ def tile_picked_haar_gelu_p_kernel(tc, x_words, x_scales, w1, w2, w3, offs, out)
                 out=band_codes[:].bitcast(FP8X4), scales=band_scales[:], in_=band_bf16[:].rearrange("p b m j -> p (b m j)")
             )
 
-        halves = {}
         quantized = {}
 
         def haar(c):
@@ -155,16 +188,16 @@ def tile_picked_haar_gelu_p_kernel(tc, x_words, x_scales, w1, w2, w3, offs, out)
             nc.sync.dma_start(out[:, lo * GROUP : hi * GROUP], result[:])
 
         last = len(CHUNKS) - 1
-        for c, (lo, hi) in enumerate(CHUNKS):
-            if c == last:
-                round_band_weights()
-            for g in range(lo, hi):
-                first_layer(g)
-                first_layer(PAIR_GROUPS + g)
-        for c in range(len(CHUNKS)):
+        for g in (0, 1, 6, 7, 2, 8, 3, 9, 4, 10):
+            first_layer(g)
+        first_layer_by_rows(CHUNKS[last][0])
+        first_layer_by_rows(PAIR_GROUPS + CHUNKS[last][0])
+        haar_by_transposes(last)
+        for c in range(last):
             haar(c)
             if c == last - 1:
                 quantize_band_weights()
             quantize_bands(c)
+        quantize_bands(last)
         for c in range(len(CHUNKS)):
             second_layer(c)

@@ -24,7 +24,7 @@ GROUP = 128
 GROUPS = S // GROUP
 PAIR_GROUPS = V // GROUP
 SLICE = 512
-CHUNKS = ((0, 1), (1, 3), (3, 5), (5, 6))
+CHUNKS = ((0, 1), (1, 3), (3, 4), (4, 5), (5, 6))
 
 
 def tile_picked_haar_gelu_p_kernel(tc, x_words, x_scales, w1, w2, w3, offs, out):
@@ -32,8 +32,8 @@ def tile_picked_haar_gelu_p_kernel(tc, x_words, x_scales, w1, w2, w3, offs, out)
     with ExitStack() as ctx:
         lists = ctx.enter_context(tc.tile_pool(name="lists", bufs=1))
         keep = ctx.enter_context(tc.tile_pool(name="keep", bufs=1))
-        hidden_psum = ctx.enter_context(tc.psum_pool(name="hidden_psum", bufs=5))
-        out_psum = ctx.enter_context(tc.psum_pool(name="out_psum", bufs=3))
+        hidden_psum = ctx.enter_context(tc.psum_pool(name="hidden_psum", bufs=6))
+        band_psum = ctx.enter_context(tc.psum_pool(name="band_psum", bufs=2))
 
         offsets = lists.tile([P, S // 16], U16, name="offsets")
         scale_table = keep.tile([P, T], U8, name="scale_table", align_bytes=64)
@@ -62,8 +62,8 @@ def tile_picked_haar_gelu_p_kernel(tc, x_words, x_scales, w1, w2, w3, offs, out)
         w1_scales = keep.tile([P, H], U8, name="w1_scales", align_bytes=64)
         dealt = w1_bf16[:].rearrange("p t m j -> p m t j")
         rows = w1_raw[:].rearrange("p j (m t) -> p m t j", t=PACK)
-        nc.scalar.copy(dealt[:, :96], rows[:, :96])
-        nc.vector.tensor_copy(dealt[:, 96:], rows[:, 96:])
+        nc.scalar.copy(dealt[:, :64], rows[:, :64])
+        nc.vector.tensor_copy(dealt[:, 64:], rows[:, 64:])
         nc.vector.quantize_mx(
             out=w1_codes[:].bitcast(FP8X4), scales=w1_scales[:], in_=w1_bf16[:].rearrange("p t m j -> p (t m j)")
         )
@@ -115,14 +115,11 @@ def tile_picked_haar_gelu_p_kernel(tc, x_words, x_scales, w1, w2, w3, offs, out)
             )
             nc.scalar.activation(hidden[:, g, :], bank[:], GELU)
 
-        def haar_by_transposes(c):
+        def haar_by_transposes(c, negated):
             g = CHUNKS[c][0]
-            negated = keep.tile([P, H], F32, name="negated")
-            nc.scalar.activation(negated[:], hidden[:, PAIR_GROUPS + g, :], COPY, scale=-1.0)
-            round_band_weights()
             bands = keep.tile([P, 2, H], BF16, name=f"bands{c}", align_bytes=64)
             for b, second in enumerate((hidden[:, PAIR_GROUPS + g, :], negated[:])):
-                bank = hidden_psum.tile([P, PACK, GROUP], F32, name="hidden_bank")
+                bank = band_psum.tile([P, PACK, GROUP], F32, name="band_bank")
                 for t in range(PACK):
                     cols = slice(t * P, (t + 1) * P)
                     nc.tensor.matmul(bank[:, t, :], hidden[:, g, cols], identity[:], start=True, stop=False, is_transpose=True)
@@ -152,10 +149,10 @@ def tile_picked_haar_gelu_p_kernel(tc, x_words, x_scales, w1, w2, w3, offs, out)
             lo, hi = CHUNKS[c]
             width = (hi - lo) * GROUP
             bands = keep.tile([P, 2, width * PACK], BF16, name=f"bands{c}", align_bytes=64)
-            first = hidden[:, lo:hi, :].rearrange("p g n -> p (g n)")
-            second = hidden[:, PAIR_GROUPS + lo : PAIR_GROUPS + hi, :].rearrange("p g n -> p (g n)")
-            nc.vector.tensor_tensor(bands[:, 0, :], first, second, ADD)
-            nc.vector.tensor_tensor(bands[:, 1, :], first, second, SUBTRACT)
+            for g in range(lo, hi):
+                cols = slice((g - lo) * H, (g - lo + 1) * H)
+                nc.vector.tensor_tensor(bands[:, 0, cols], hidden[:, g, :], hidden[:, PAIR_GROUPS + g, :], ADD)
+                nc.vector.tensor_tensor(bands[:, 1, cols], hidden[:, g, :], hidden[:, PAIR_GROUPS + g, :], SUBTRACT)
             halves[c] = bands
 
         def quantize_bands(c):
@@ -172,7 +169,7 @@ def tile_picked_haar_gelu_p_kernel(tc, x_words, x_scales, w1, w2, w3, offs, out)
             lo, hi = CHUNKS[c]
             width = (hi - lo) * GROUP
             codes, scales = quantized[c]
-            bank = out_psum.tile([P, width], F32, name="out_bank")
+            bank = hidden_psum.tile([P, width], F32, name="hidden_bank")
             for b in range(2):
                 nc.tensor.matmul_mx(
                     out=bank[:],
@@ -188,15 +185,24 @@ def tile_picked_haar_gelu_p_kernel(tc, x_words, x_scales, w1, w2, w3, offs, out)
             nc.sync.dma_start(out[:, lo * GROUP : hi * GROUP], result[:])
 
         last = len(CHUNKS) - 1
-        for g in (0, 1, 6, 7, 2, 8, 3, 9, 4, 10):
+        turned = CHUNKS[last][0]
+        negated = keep.tile([P, H], F32, name="negated")
+        for g in (0, 1, 6, 7):
             first_layer(g)
-        first_layer_by_rows(CHUNKS[last][0])
-        first_layer_by_rows(PAIR_GROUPS + CHUNKS[last][0])
-        haar_by_transposes(last)
+        round_band_weights()
+        for g in (2, 8):
+            first_layer(g)
+        first_layer_by_rows(turned)
+        first_layer_by_rows(PAIR_GROUPS + turned)
+        for g in (3, 9):
+            first_layer(g)
+        nc.vector.tensor_scalar_mul(negated[:], hidden[:, PAIR_GROUPS + turned, :], -1.0)
+        for g in (4, 10):
+            first_layer(g)
+        haar_by_transposes(last, negated)
+        quantize_band_weights()
         for c in range(last):
             haar(c)
-            if c == last - 1:
-                quantize_band_weights()
             quantize_bands(c)
         quantize_bands(last)
         for c in range(len(CHUNKS)):

@@ -44,10 +44,6 @@ def tile_picked_haar_gelu_p_kernel(tc, x_words, x_scales, w1, w2, w3, offs, out)
         nc.sync.dma_start(w1_raw[:], w1.rearrange("(p j) c -> p j c", j=PACK))
         nc.sync.dma_start(word_table[:].bitcast(I32), x_words[0].rearrange("p n t -> p (n t)").bitcast(I32))
 
-        warm = keep.tile([P, 2], F32, name="warm")
-        nc.vector.memset(warm[:, 0:1], 0.0)
-        nc.scalar.activation(warm[:, 1:2], warm[:, 0:1], GELU)
-
         for first, last in ((0, 16), (32, 64), (64, P)):
             nc.vector.memset(scale_table[first:last, :].bitcast(I32), 0)
         picked_rows = keep.tile([P, S], U8, name="picked_rows", align_bytes=64)
@@ -62,8 +58,7 @@ def tile_picked_haar_gelu_p_kernel(tc, x_words, x_scales, w1, w2, w3, offs, out)
         w1_scales = keep.tile([P, H], U8, name="w1_scales", align_bytes=64)
         dealt = w1_bf16[:].rearrange("p t m j -> p m t j")
         rows = w1_raw[:].rearrange("p j (m t) -> p m t j", t=PACK)
-        nc.scalar.copy(dealt[:, :64], rows[:, :64])
-        nc.vector.tensor_copy(dealt[:, 64:], rows[:, 64:])
+        nc.vector.tensor_copy(dealt, rows)
         nc.vector.quantize_mx(
             out=w1_codes[:].bitcast(FP8X4), scales=w1_scales[:], in_=w1_bf16[:].rearrange("p t m j -> p (t m j)")
         )

@@ -24,7 +24,10 @@ GROUP = 128
 GROUPS = S // GROUP
 PAIR_GROUPS = V // GROUP
 SLICE = 512
-CHUNKS = ((0, 1), (1, 3), (3, 4), (4, 5), (5, 6))
+HALF = H // 2
+SCALAR_SHARE = 24
+DIRECT = (0, 1, 2, 3)
+TURNED = (4, 5)
 
 
 def tile_picked_haar_gelu_p_kernel(tc, x_words, x_scales, w1, w2, w3, offs, out):
@@ -32,48 +35,72 @@ def tile_picked_haar_gelu_p_kernel(tc, x_words, x_scales, w1, w2, w3, offs, out)
     with ExitStack() as ctx:
         lists = ctx.enter_context(tc.tile_pool(name="lists", bufs=1))
         keep = ctx.enter_context(tc.tile_pool(name="keep", bufs=1))
-        hidden_psum = ctx.enter_context(tc.psum_pool(name="hidden_psum", bufs=6))
-        band_psum = ctx.enter_context(tc.psum_pool(name="band_psum", bufs=2))
+        hidden_psum = ctx.enter_context(tc.psum_pool(name="hidden_psum", bufs=4))
+        band_psum = ctx.enter_context(tc.psum_pool(name="band_psum", bufs=4))
 
         offsets = lists.tile([P, S // 16], U16, name="offsets")
-        scale_table = keep.tile([P, T], U8, name="scale_table", align_bytes=64)
+        scale_table = keep.tile([P, T], U8, name="scale_table", tag="table_then_band", align_bytes=64)
         word_table = keep.tile([P, T], U32, name="word_table", align_bytes=64)
-        w1_raw = keep.tile([P, PACK, H], F32, name="w1_raw", tag="raw_weights")
-        nc.sync.dma_start(scale_table[16:32, :].bitcast(I32), x_scales[0].bitcast(I32))
+        nc.sync.dma_start(scale_table[P - 16 : P, :].bitcast(I32), x_scales[0].bitcast(I32))
         nc.sync.dma_start(offsets[:], offs)
-        nc.sync.dma_start(w1_raw[:], w1.rearrange("(p j) c -> p j c", j=PACK))
         nc.sync.dma_start(word_table[:].bitcast(I32), x_words[0].rearrange("p n t -> p (n t)").bitcast(I32))
+        w1_raw = []
+        for h in range(2):
+            raw = keep.tile([P, PACK, HALF], F32, name=f"w1_raw{h}")
+            nc.sync.dma_start(raw[:], w1[:, h * HALF : (h + 1) * HALF].rearrange("(p j) c -> p j c", j=PACK))
+            w1_raw.append(raw)
 
-        for first, last in ((0, 16), (32, 64), (64, P)):
-            nc.vector.memset(scale_table[first:last, :].bitcast(I32), 0)
+        identity = keep.tile([P, P], F32, name="identity")
+        make_identity(nc, identity[:])
+        warm = keep.tile([P, 1], F32, name="warm")
+        nc.scalar.activation(warm[:], identity[:, 0:1], GELU)
+
+        nc.vector.memset(scale_table[0 : P - 16, :].bitcast(I32), 0)
         picked_rows = keep.tile([P, S], U8, name="picked_rows", align_bytes=64)
         picked_scales = keep.tile([P, S], U8, name="picked_scales", align_bytes=64)
         nc.vector.memset(picked_scales[:].bitcast(I32), 0)
         nc.vector.tensor_copy(picked_rows[:], scale_table[:].indirect(offsets[:]))
         for r in range(4):
-            nc.sync.dma_start(picked_scales[r:P:32, :].bitcast(I32), picked_rows[16 + r : 32 : 4, :].bitcast(I32))
+            nc.sync.dma_start(picked_scales[r:P:32, :].bitcast(I32), picked_rows[P - 16 + r : P : 4, :].bitcast(I32))
 
-        w1_bf16 = keep.tile([P, PACK, P, PACK], BF16, name="w1_bf16", align_bytes=64)
-        w1_codes = keep.tile([P, H], U32, name="w1_codes", align_bytes=64)
-        w1_scales = keep.tile([P, H], U8, name="w1_scales", align_bytes=64)
-        dealt = w1_bf16[:].rearrange("p t m j -> p m t j")
-        rows = w1_raw[:].rearrange("p j (m t) -> p m t j", t=PACK)
-        nc.vector.tensor_copy(dealt, rows)
-        nc.vector.quantize_mx(
-            out=w1_codes[:].bitcast(FP8X4), scales=w1_scales[:], in_=w1_bf16[:].rearrange("p t m j -> p (t m j)")
-        )
-
-        band_raw = keep.tile([P, 2, PACK, N], F32, name="band_raw", tag="raw_weights")
+        band_raw = keep.tile([P, 2, PACK, N], F32, name="band_raw", tag="table_then_band", align_bytes=64)
         for b, w in enumerate((w2, w3)):
             nc.sync.dma_start(band_raw[:, b], w.rearrange("(p j) m -> p j m", j=PACK))
 
-        picked_words = []
-        for s in range(S // SLICE):
-            picked = keep.tile([P, SLICE], U32, name=f"picked_words{s}", align_bytes=64)
-            nc.vector.tensor_copy(picked[:], word_table[:].indirect(offsets[:, s * SLICE // 16 : (s + 1) * SLICE // 16]))
-            picked_words.append(picked)
+        picked_words = {}
 
-        halves = {}
+        def gather_words(s, tag):
+            picked = keep.tile([P, SLICE], U32, name=f"picked_words{s}", tag=tag, align_bytes=64)
+            nc.vector.tensor_copy(picked[:], word_table[:].indirect(offsets[:, s * SLICE // 16 : (s + 1) * SLICE // 16]))
+            picked_words[s] = picked
+
+        gather_words(0, "picked0")
+        gather_words(1, "picked1")
+
+        w1_bf16 = [
+            keep.tile([P, 2, P, PACK], BF16, name=f"w1_bf16_{u}", tag=f"w1_bf16_{u}", align_bytes=64) for u in range(2)
+        ]
+        w1_codes = keep.tile([P, H], U32, name="w1_codes", align_bytes=64)
+        w1_scales = keep.tile([P, H], U8, name="w1_scales", align_bytes=64)
+
+        def round_w1(copy, h, lo, hi):
+            rows = w1_raw[h][:].rearrange("p j (m t) -> p m t j", t=PACK)
+            for u in range(2):
+                dealt = w1_bf16[u][:].rearrange("p t m j -> p m t j")
+                copy(dealt[:, 64 * h + lo : 64 * h + hi], rows[:, lo:hi, 2 * u : 2 * u + 2, :])
+
+        round_w1(nc.scalar.copy, 0, 0, 64)
+        round_w1(nc.scalar.copy, 1, 0, SCALAR_SHARE)
+        round_w1(nc.vector.tensor_copy, 1, SCALAR_SHARE, 64)
+        for u in range(2):
+            cols = slice(u * HALF, (u + 1) * HALF)
+            nc.vector.quantize_mx(
+                out=w1_codes[:, cols].bitcast(FP8X4),
+                scales=w1_scales[:, cols],
+                in_=w1_bf16[u][:].rearrange("p t m j -> p (t m j)"),
+            )
+        gather_words(2, "w1_bf16_0")
+
         hidden = keep.tile([P, GROUPS, GROUP * PACK], F32, name="hidden")
 
         def first_layer(g):
@@ -93,9 +120,6 @@ def tile_picked_haar_gelu_p_kernel(tc, x_words, x_scales, w1, w2, w3, offs, out)
                 hidden[:, g, :].rearrange("p (n t) -> p n t", t=PACK), bank[:].rearrange("p t n -> p n t"), GELU
             )
 
-        identity = keep.tile([P, P], F32, name="identity")
-        make_identity(nc, identity[:])
-
         def first_layer_by_rows(g):
             s, first = divmod(g * GROUP, SLICE)
             bank = hidden_psum.tile([P, H], F32, name="hidden_bank")
@@ -110,95 +134,97 @@ def tile_picked_haar_gelu_p_kernel(tc, x_words, x_scales, w1, w2, w3, offs, out)
             )
             nc.scalar.activation(hidden[:, g, :], bank[:], GELU)
 
-        def haar_by_transposes(c, negated):
-            g = CHUNKS[c][0]
-            bands = keep.tile([P, 2, H], BF16, name=f"bands{c}", align_bytes=64)
+        bands = [keep.tile([P, 2, H], BF16, name=f"bands{g}", align_bytes=64) for g in range(PAIR_GROUPS)]
+        turned_banks = {}
+
+        def turn(g):
+            negated = keep.tile([P, H], F32, name=f"negated{g}")
+            nc.vector.tensor_scalar_mul(negated[:], hidden[:, PAIR_GROUPS + g, :], -1.0)
             for b, second in enumerate((hidden[:, PAIR_GROUPS + g, :], negated[:])):
                 bank = band_psum.tile([P, PACK, GROUP], F32, name="band_bank")
                 for t in range(PACK):
                     cols = slice(t * P, (t + 1) * P)
                     nc.tensor.matmul(bank[:, t, :], hidden[:, g, cols], identity[:], start=True, stop=False, is_transpose=True)
                     nc.tensor.matmul(bank[:, t, :], second[:, cols], identity[:], start=False, stop=True, is_transpose=True)
-                nc.scalar.copy(bands[:, b, :].rearrange("p (n t) -> p n t", t=PACK), bank[:].rearrange("p t n -> p n t"))
-            halves[c] = bands
+                turned_banks[g, b] = bank
+
+        def empty_turned(g, b, copy):
+            copy(bands[g][:, b, :].rearrange("p (n t) -> p n t", t=PACK), turned_banks[g, b][:].rearrange("p t n -> p n t"))
 
         band_bf16 = keep.tile([P, 2, N, PACK], BF16, name="band_bf16", align_bytes=64)
         band_codes = keep.tile([P, 2 * N], U32, name="band_codes", align_bytes=64)
         band_scales = keep.tile([P, 2 * N], U8, name="band_scales", align_bytes=64)
 
-        def round_band_weights():
+        def band_weights():
             for b in range(2):
-                nc.scalar.copy(
+                nc.vector.tensor_copy(
                     band_bf16[:, b].rearrange("p (c i) j -> p c j i", i=PACK),
                     band_raw[:, b].rearrange("p j (c i) -> p c j i", i=PACK),
                 )
-
-        def quantize_band_weights():
             nc.vector.quantize_mx(
                 out=band_codes[:].bitcast(FP8X4), scales=band_scales[:], in_=band_bf16[:].rearrange("p b m j -> p (b m j)")
             )
 
+        def haar(g):
+            nc.vector.tensor_tensor(bands[g][:, 0, :], hidden[:, g, :], hidden[:, PAIR_GROUPS + g, :], ADD)
+            nc.vector.tensor_tensor(bands[g][:, 1, :], hidden[:, g, :], hidden[:, PAIR_GROUPS + g, :], SUBTRACT)
+
         quantized = {}
 
-        def haar(c):
-            lo, hi = CHUNKS[c]
-            width = (hi - lo) * GROUP
-            bands = keep.tile([P, 2, width * PACK], BF16, name=f"bands{c}", align_bytes=64)
-            for g in range(lo, hi):
-                cols = slice((g - lo) * H, (g - lo + 1) * H)
-                nc.vector.tensor_tensor(bands[:, 0, cols], hidden[:, g, :], hidden[:, PAIR_GROUPS + g, :], ADD)
-                nc.vector.tensor_tensor(bands[:, 1, cols], hidden[:, g, :], hidden[:, PAIR_GROUPS + g, :], SUBTRACT)
-            halves[c] = bands
-
-        def quantize_bands(c):
-            lo, hi = CHUNKS[c]
-            width = (hi - lo) * GROUP
-            bands = halves[c]
-            codes = keep.tile([P, 2, width], U32, name=f"codes{c}", align_bytes=64)
-            scales = keep.tile([P, 2, width], U8, name=f"scales{c}", align_bytes=64)
-            for b in range(2):
-                nc.vector.quantize_mx(out=codes[:, b, :].bitcast(FP8X4), scales=scales[:, b, :], in_=bands[:, b, :])
-            quantized[c] = (codes, scales)
-
-        def second_layer(c):
-            lo, hi = CHUNKS[c]
-            width = (hi - lo) * GROUP
-            codes, scales = quantized[c]
-            bank = hidden_psum.tile([P, width], F32, name="hidden_bank")
-            for b in range(2):
-                nc.tensor.matmul_mx(
-                    out=bank[:],
-                    lhsT=band_codes[:, b * N : (b + 1) * N].bitcast(FP8X4),
-                    lhsT_scale=band_scales[:, b * N : (b + 1) * N],
-                    rhs=codes[:, b, :].bitcast(FP8X4),
-                    rhs_scale=scales[:, b, :],
-                    start=(b == 0),
-                    stop=(b == 1),
+        def quantize_bands(g, calls=((0, 2),)):
+            codes = keep.tile([P, 2, GROUP], U32, name=f"codes{g}", align_bytes=64)
+            scales = keep.tile([P, 2, GROUP], U8, name=f"scales{g}", align_bytes=64)
+            for lo, hi in calls:
+                nc.vector.quantize_mx(
+                    out=codes[:, lo:hi, :].rearrange("p b n -> p (b n)").bitcast(FP8X4),
+                    scales=scales[:, lo:hi, :].rearrange("p b n -> p (b n)"),
+                    in_=bands[g][:, lo:hi, :].rearrange("p b c -> p (b c)"),
                 )
-            result = keep.tile([P, width], F32, name=f"result{c}")
+            quantized[g] = (codes, scales)
+
+        def second_layer(lo, hi):
+            width = (hi - lo) * GROUP
+            bank = hidden_psum.tile([P, width], F32, name="hidden_bank")
+            for g in range(lo, hi):
+                codes, scales = quantized[g]
+                for b in range(2):
+                    nc.tensor.matmul_mx(
+                        out=bank[:, (g - lo) * GROUP : (g - lo + 1) * GROUP],
+                        lhsT=band_codes[:, b * N : (b + 1) * N].bitcast(FP8X4),
+                        lhsT_scale=band_scales[:, b * N : (b + 1) * N],
+                        rhs=codes[:, b, :].bitcast(FP8X4),
+                        rhs_scale=scales[:, b, :],
+                        start=(b == 0),
+                        stop=(b == 1),
+                    )
+            result = keep.tile([P, width], F32, name=f"result{lo}")
             nc.scalar.activation(result[:], bank[:], COPY, scale=0.5)
             nc.sync.dma_start(out[:, lo * GROUP : hi * GROUP], result[:])
 
-        last = len(CHUNKS) - 1
-        turned = CHUNKS[last][0]
-        negated = keep.tile([P, H], F32, name="negated")
-        for g in (0, 1, 6, 7):
-            first_layer(g)
-        round_band_weights()
-        for g in (2, 8):
-            first_layer(g)
-        first_layer_by_rows(turned)
-        first_layer_by_rows(PAIR_GROUPS + turned)
-        for g in (3, 9):
-            first_layer(g)
-        nc.vector.tensor_scalar_mul(negated[:], hidden[:, PAIR_GROUPS + turned, :], -1.0)
-        for g in (4, 10):
-            first_layer(g)
-        haar_by_transposes(last, negated)
-        quantize_band_weights()
-        for c in range(last):
-            haar(c)
-            quantize_bands(c)
-        quantize_bands(last)
-        for c in range(len(CHUNKS)):
-            second_layer(c)
+        def pair(g):
+            layer = first_layer_by_rows if g in TURNED else first_layer
+            layer(g)
+            layer(PAIR_GROUPS + g)
+
+        for g in (0, 4, 1, 5, 2, 3):
+            pair(g)
+        band_weights()
+        haar(0)
+        turn(4)
+        haar(1)
+        quantize_bands(0)
+        turn(5)
+        haar(2)
+        quantize_bands(1)
+        haar(3)
+        quantize_bands(2)
+        for g in TURNED:
+            for b in range(2):
+                empty_turned(g, b, nc.scalar.copy)
+        quantize_bands(4)
+        second_layer(0, 2)
+        quantize_bands(3)
+        second_layer(2, 4)
+        quantize_bands(5, ((0, 1), (1, 2)))
+        second_layer(4, 5)
+        second_layer(5, 6)

@@ -25,9 +25,8 @@ GROUPS = S // GROUP
 PAIR_GROUPS = V // GROUP
 SLICE = 512
 HALF = H // 2
-SCALAR_SHARE = 24
-DIRECT = (0, 1, 2, 3)
-TURNED = (4, 5)
+SCALAR_SHARE = 96
+TURNED = (0, 5)
 
 
 def tile_picked_haar_gelu_p_kernel(tc, x_words, x_scales, w1, w2, w3, offs, out):
@@ -35,73 +34,61 @@ def tile_picked_haar_gelu_p_kernel(tc, x_words, x_scales, w1, w2, w3, offs, out)
     with ExitStack() as ctx:
         lists = ctx.enter_context(tc.tile_pool(name="lists", bufs=1))
         keep = ctx.enter_context(tc.tile_pool(name="keep", bufs=1))
+        reused = ctx.enter_context(tc.tile_pool(name="reused", bufs=1))
         hidden_psum = ctx.enter_context(tc.psum_pool(name="hidden_psum", bufs=4))
         band_psum = ctx.enter_context(tc.psum_pool(name="band_psum", bufs=4))
 
         offsets = lists.tile([P, S // 16], U16, name="offsets")
-        scale_table = keep.tile([P, T], U8, name="scale_table", tag="table_then_band", align_bytes=64)
+        scale_table = reused.tile([P, T], U8, name="scale_table", offset=0, align_bytes=64)
         word_table = keep.tile([P, T], U32, name="word_table", align_bytes=64)
-        nc.sync.dma_start(scale_table[P - 16 : P, :].bitcast(I32), x_scales[0].bitcast(I32))
+        w1_raw = keep.tile([P, PACK, H], F32, name="w1_raw")
+        warm = keep.tile([P, 2], F32, name="warm")
+        nc.vector.memset(warm[:, 0:1], 0.0)
+        nc.scalar.activation(warm[:, 1:2], warm[:, 0:1], GELU)
+        nc.vector.memset(scale_table[:, : T // 2].bitcast(I32), 0)
+        nc.gpsimd.memset(scale_table[:, T // 2 :].bitcast(I32), 0)
+        w1_rows = w1.rearrange("(p j) c -> p j c", j=PACK)
         nc.sync.dma_start(offsets[:], offs)
+        nc.sync.dma_start(w1_raw[:, 0:2], w1_rows[:, 0:2])
+        nc.sync.dma_start(scale_table[32:96:4, :].bitcast(I32), x_scales[0].bitcast(I32))
+        nc.sync.dma_start(w1_raw[:, 2:4], w1_rows[:, 2:4])
         nc.sync.dma_start(word_table[:].bitcast(I32), x_words[0].rearrange("p n t -> p (n t)").bitcast(I32))
-        w1_raw = []
-        for h in range(2):
-            raw = keep.tile([P, PACK, HALF], F32, name=f"w1_raw{h}")
-            nc.sync.dma_start(raw[:], w1[:, h * HALF : (h + 1) * HALF].rearrange("(p j) c -> p j c", j=PACK))
-            w1_raw.append(raw)
+        w2_raw = reused.tile([P, PACK, N], F32, name="w2_raw", offset=T, align_bytes=64)
+        nc.sync.dma_start(w2_raw[:], w2.rearrange("(p j) m -> p j m", j=PACK))
 
         identity = keep.tile([P, P], F32, name="identity")
         make_identity(nc, identity[:])
-        warm = keep.tile([P, 1], F32, name="warm")
-        nc.scalar.activation(warm[:], identity[:, 0:1], GELU)
 
-        nc.vector.memset(scale_table[0 : P - 16, :].bitcast(I32), 0)
         picked_rows = keep.tile([P, S], U8, name="picked_rows", align_bytes=64)
         picked_scales = keep.tile([P, S], U8, name="picked_scales", align_bytes=64)
         nc.vector.memset(picked_scales[:].bitcast(I32), 0)
         nc.vector.tensor_copy(picked_rows[:], scale_table[:].indirect(offsets[:]))
         for r in range(4):
-            nc.sync.dma_start(picked_scales[r:P:32, :].bitcast(I32), picked_rows[P - 16 + r : P : 4, :].bitcast(I32))
+            nc.sync.dma_start(picked_scales[r:P:32, :].bitcast(I32), picked_rows[32 + 4 * r : 96 : 16, :].bitcast(I32))
 
-        band_raw = keep.tile([P, 2, PACK, N], F32, name="band_raw", tag="table_then_band", align_bytes=64)
-        for b, w in enumerate((w2, w3)):
-            nc.sync.dma_start(band_raw[:, b], w.rearrange("(p j) m -> p j m", j=PACK))
+        w3_raw = reused.tile([P, PACK, N], F32, name="w3_raw", offset=0, align_bytes=64)
+        nc.sync.dma_start(w3_raw[:], w3.rearrange("(p j) m -> p j m", j=PACK))
+        band_raw = [w2_raw, w3_raw]
 
-        picked_words = {}
-
-        def gather_words(s, tag):
-            picked = keep.tile([P, SLICE], U32, name=f"picked_words{s}", tag=tag, align_bytes=64)
-            nc.vector.tensor_copy(picked[:], word_table[:].indirect(offsets[:, s * SLICE // 16 : (s + 1) * SLICE // 16]))
-            picked_words[s] = picked
-
-        gather_words(0, "picked0")
-        gather_words(1, "picked1")
-
-        w1_bf16 = [
-            keep.tile([P, 2, P, PACK], BF16, name=f"w1_bf16_{u}", tag=f"w1_bf16_{u}", align_bytes=64) for u in range(2)
-        ]
+        w1_bf16 = keep.tile([P, PACK, P, PACK], BF16, name="w1_bf16", align_bytes=64)
         w1_codes = keep.tile([P, H], U32, name="w1_codes", align_bytes=64)
         w1_scales = keep.tile([P, H], U8, name="w1_scales", align_bytes=64)
+        dealt = w1_bf16[:].rearrange("p t m j -> p m t j")
+        rows = w1_raw[:].rearrange("p j (m t) -> p m t j", t=PACK)
+        nc.scalar.copy(dealt[:, :SCALAR_SHARE], rows[:, :SCALAR_SHARE])
+        nc.vector.tensor_copy(dealt[:, SCALAR_SHARE:], rows[:, SCALAR_SHARE:])
+        nc.vector.quantize_mx(
+            out=w1_codes[:].bitcast(FP8X4), scales=w1_scales[:], in_=w1_bf16[:].rearrange("p t m j -> p (t m j)")
+        )
 
-        def round_w1(copy, h, lo, hi):
-            rows = w1_raw[h][:].rearrange("p j (m t) -> p m t j", t=PACK)
-            for u in range(2):
-                dealt = w1_bf16[u][:].rearrange("p t m j -> p m t j")
-                copy(dealt[:, 64 * h + lo : 64 * h + hi], rows[:, lo:hi, 2 * u : 2 * u + 2, :])
+        picked_words = []
+        for s in range(S // SLICE):
+            picked = keep.tile([P, SLICE], U32, name=f"picked_words{s}", align_bytes=64)
+            nc.vector.tensor_copy(picked[:], word_table[:].indirect(offsets[:, s * SLICE // 16 : (s + 1) * SLICE // 16]))
+            picked_words.append(picked)
 
-        round_w1(nc.scalar.copy, 0, 0, 64)
-        round_w1(nc.scalar.copy, 1, 0, SCALAR_SHARE)
-        round_w1(nc.vector.tensor_copy, 1, SCALAR_SHARE, 64)
-        for u in range(2):
-            cols = slice(u * HALF, (u + 1) * HALF)
-            nc.vector.quantize_mx(
-                out=w1_codes[:, cols].bitcast(FP8X4),
-                scales=w1_scales[:, cols],
-                in_=w1_bf16[u][:].rearrange("p t m j -> p (t m j)"),
-            )
-        gather_words(2, "w1_bf16_0")
-
-        hidden = keep.tile([P, GROUPS, GROUP * PACK], F32, name="hidden")
+        hidden = [reused.tile([P, H], F32, name="hidden0", offset=T, align_bytes=64)]
+        hidden.extend(keep.tile([P, H], F32, name=f"hidden{g}") for g in range(1, GROUPS))
 
         def first_layer(g):
             s, first = divmod(g * GROUP, SLICE)
@@ -117,34 +104,36 @@ def tile_picked_haar_gelu_p_kernel(tc, x_words, x_scales, w1, w2, w3, offs, out)
                     stop=True,
                 )
             nc.scalar.activation(
-                hidden[:, g, :].rearrange("p (n t) -> p n t", t=PACK), bank[:].rearrange("p t n -> p n t"), GELU
+                hidden[g][:].rearrange("p (n t) -> p n t", t=PACK), bank[:].rearrange("p t n -> p n t"), GELU
             )
 
-        def first_layer_by_rows(g):
+        def first_layer_by_rows(g, width=H):
             s, first = divmod(g * GROUP, SLICE)
-            bank = hidden_psum.tile([P, H], F32, name="hidden_bank")
-            nc.tensor.matmul_mx(
-                out=bank[:],
-                lhsT=picked_words[s][:, first : first + GROUP].bitcast(FP8X4),
-                lhsT_scale=picked_scales[:, g * GROUP : (g + 1) * GROUP],
-                rhs=w1_codes[:].bitcast(FP8X4),
-                rhs_scale=w1_scales[:],
-                start=True,
-                stop=True,
-            )
-            nc.scalar.activation(hidden[:, g, :], bank[:], GELU)
+            for lo in range(0, H, width):
+                cols = slice(lo, lo + width)
+                bank = hidden_psum.tile([P, width], F32, name="hidden_bank")
+                nc.tensor.matmul_mx(
+                    out=bank[:],
+                    lhsT=picked_words[s][:, first : first + GROUP].bitcast(FP8X4),
+                    lhsT_scale=picked_scales[:, g * GROUP : (g + 1) * GROUP],
+                    rhs=w1_codes[:, cols].bitcast(FP8X4),
+                    rhs_scale=w1_scales[:, cols],
+                    start=True,
+                    stop=True,
+                )
+                nc.scalar.activation(hidden[g][:, cols], bank[:], GELU)
 
         bands = [keep.tile([P, 2, H], BF16, name=f"bands{g}", align_bytes=64) for g in range(PAIR_GROUPS)]
         turned_banks = {}
 
         def turn(g):
             negated = keep.tile([P, H], F32, name=f"negated{g}")
-            nc.vector.tensor_scalar_mul(negated[:], hidden[:, PAIR_GROUPS + g, :], -1.0)
-            for b, second in enumerate((hidden[:, PAIR_GROUPS + g, :], negated[:])):
+            nc.vector.tensor_scalar_mul(negated[:], hidden[PAIR_GROUPS + g][:], -1.0)
+            for b, second in enumerate((hidden[PAIR_GROUPS + g], negated)):
                 bank = band_psum.tile([P, PACK, GROUP], F32, name="band_bank")
                 for t in range(PACK):
                     cols = slice(t * P, (t + 1) * P)
-                    nc.tensor.matmul(bank[:, t, :], hidden[:, g, cols], identity[:], start=True, stop=False, is_transpose=True)
+                    nc.tensor.matmul(bank[:, t, :], hidden[g][:, cols], identity[:], start=True, stop=False, is_transpose=True)
                     nc.tensor.matmul(bank[:, t, :], second[:, cols], identity[:], start=False, stop=True, is_transpose=True)
                 turned_banks[g, b] = bank
 
@@ -155,19 +144,20 @@ def tile_picked_haar_gelu_p_kernel(tc, x_words, x_scales, w1, w2, w3, offs, out)
         band_codes = keep.tile([P, 2 * N], U32, name="band_codes", align_bytes=64)
         band_scales = keep.tile([P, 2 * N], U8, name="band_scales", align_bytes=64)
 
-        def band_weights():
-            for b in range(2):
-                nc.vector.tensor_copy(
-                    band_bf16[:, b].rearrange("p (c i) j -> p c j i", i=PACK),
-                    band_raw[:, b].rearrange("p j (c i) -> p c j i", i=PACK),
-                )
+        def round_band_weights(b, copy):
+            copy(
+                band_bf16[:, b].rearrange("p (c i) j -> p c j i", i=PACK),
+                band_raw[b][:].rearrange("p j (c i) -> p c j i", i=PACK),
+            )
+
+        def quantize_band_weights():
             nc.vector.quantize_mx(
                 out=band_codes[:].bitcast(FP8X4), scales=band_scales[:], in_=band_bf16[:].rearrange("p b m j -> p (b m j)")
             )
 
         def haar(g):
-            nc.vector.tensor_tensor(bands[g][:, 0, :], hidden[:, g, :], hidden[:, PAIR_GROUPS + g, :], ADD)
-            nc.vector.tensor_tensor(bands[g][:, 1, :], hidden[:, g, :], hidden[:, PAIR_GROUPS + g, :], SUBTRACT)
+            nc.vector.tensor_tensor(bands[g][:, 0, :], hidden[g][:], hidden[PAIR_GROUPS + g][:], ADD)
+            nc.vector.tensor_tensor(bands[g][:, 1, :], hidden[g][:], hidden[PAIR_GROUPS + g][:], SUBTRACT)
 
         quantized = {}
 
@@ -182,7 +172,7 @@ def tile_picked_haar_gelu_p_kernel(tc, x_words, x_scales, w1, w2, w3, offs, out)
                 )
             quantized[g] = (codes, scales)
 
-        def second_layer(lo, hi):
+        def second_layer(lo, hi, halve):
             width = (hi - lo) * GROUP
             bank = hidden_psum.tile([P, width], F32, name="hidden_bank")
             for g in range(lo, hi):
@@ -198,7 +188,7 @@ def tile_picked_haar_gelu_p_kernel(tc, x_words, x_scales, w1, w2, w3, offs, out)
                         stop=(b == 1),
                     )
             result = keep.tile([P, width], F32, name=f"result{lo}")
-            nc.scalar.activation(result[:], bank[:], COPY, scale=0.5)
+            halve(result[:], bank[:], 0.5)
             nc.sync.dma_start(out[:, lo * GROUP : hi * GROUP], result[:])
 
         def pair(g):
@@ -206,25 +196,31 @@ def tile_picked_haar_gelu_p_kernel(tc, x_words, x_scales, w1, w2, w3, offs, out)
             layer(g)
             layer(PAIR_GROUPS + g)
 
-        for g in (0, 4, 1, 5, 2, 3):
+        round_band_weights(0, nc.scalar.copy)
+        first_layer_by_rows(0, HALF)
+        first_layer(1)
+        first_layer_by_rows(PAIR_GROUPS)
+        first_layer(PAIR_GROUPS + 1)
+        for g in (5, 2, 3, 4):
             pair(g)
-        band_weights()
-        haar(0)
-        turn(4)
+        round_band_weights(1, nc.vector.tensor_copy)
+        turn(0)
+        quantize_band_weights()
         haar(1)
-        quantize_bands(0)
         turn(5)
-        haar(2)
         quantize_bands(1)
+        haar(2)
         haar(3)
         quantize_bands(2)
+        haar(4)
+        quantize_bands(3)
         for g in TURNED:
             for b in range(2):
                 empty_turned(g, b, nc.scalar.copy)
+        quantize_bands(0)
+        second_layer(1, 4, nc.scalar.mul)
         quantize_bands(4)
-        second_layer(0, 2)
-        quantize_bands(3)
-        second_layer(2, 4)
+        second_layer(0, 1, nc.scalar.mul)
         quantize_bands(5, ((0, 1), (1, 2)))
-        second_layer(4, 5)
-        second_layer(5, 6)
+        second_layer(4, 5, nc.scalar.mul)
+        second_layer(5, 6, nc.vector.tensor_scalar_mul)

@@ -26,6 +26,7 @@ PAIR_GROUPS = V // GROUP
 SLICE = 512
 HALF = H // 2
 SCALAR_SHARE = 96
+WARM_PASSES = 3
 TURNED = (0, 5)
 
 
@@ -80,6 +81,18 @@ def tile_picked_haar_gelu_p_kernel(tc, x_words, x_scales, w1, w2, w3, offs, out)
         nc.vector.quantize_mx(
             out=w1_codes[:].bitcast(FP8X4), scales=w1_scales[:], in_=w1_bf16[:].rearrange("p t m j -> p (t m j)")
         )
+
+        warm_bank = hidden_psum.tile([P, H], F32, name="hidden_bank")
+        for u in range(WARM_PASSES):
+            nc.tensor.matmul_mx(
+                out=warm_bank[:],
+                lhsT=w1_codes[:, :P].bitcast(FP8X4),
+                lhsT_scale=w1_scales[:, :P],
+                rhs=w1_codes[:].bitcast(FP8X4),
+                rhs_scale=w1_scales[:],
+                start=True,
+                stop=True,
+            )
 
         picked_words = []
         for s in range(S // SLICE):
@@ -201,19 +214,19 @@ def tile_picked_haar_gelu_p_kernel(tc, x_words, x_scales, w1, w2, w3, offs, out)
         first_layer(1)
         first_layer_by_rows(PAIR_GROUPS)
         first_layer(PAIR_GROUPS + 1)
-        for g in (5, 2, 3, 4):
+        for g in (2, 3, 5, 4):
             pair(g)
         round_band_weights(1, nc.vector.tensor_copy)
         turn(0)
         quantize_band_weights()
         haar(1)
-        turn(5)
-        quantize_bands(1)
         haar(2)
+        quantize_bands(1)
         haar(3)
         quantize_bands(2)
-        haar(4)
+        turn(5)
         quantize_bands(3)
+        haar(4)
         for g in TURNED:
             for b in range(2):
                 empty_turned(g, b, nc.scalar.copy)

@@ -36,8 +36,7 @@ def tile_picked_haar_gelu_p_kernel(tc, x_words, x_scales, w1, w2, w3, offs, out)
         lists = ctx.enter_context(tc.tile_pool(name="lists", bufs=1))
         keep = ctx.enter_context(tc.tile_pool(name="keep", bufs=1))
         reused = ctx.enter_context(tc.tile_pool(name="reused", bufs=1))
-        hidden_psum = ctx.enter_context(tc.psum_pool(name="hidden_psum", bufs=4))
-        band_psum = ctx.enter_context(tc.psum_pool(name="band_psum", bufs=4))
+        psum = ctx.enter_context(tc.psum_pool(name="psum", bufs=1))
 
         offsets = lists.tile([P, S // 16], U16, name="offsets")
         scale_table = reused.tile([P, T], U8, name="scale_table", offset=0, align_bytes=64)
@@ -82,7 +81,7 @@ def tile_picked_haar_gelu_p_kernel(tc, x_words, x_scales, w1, w2, w3, offs, out)
             out=w1_codes[:].bitcast(FP8X4), scales=w1_scales[:], in_=w1_bf16[:].rearrange("p t m j -> p (t m j)")
         )
 
-        warm_bank = hidden_psum.tile([P, H], F32, name="hidden_bank")
+        warm_bank = psum.tile([P, H], F32, name="warm_bank", tag="bank7")
         for u in range(WARM_PASSES):
             nc.tensor.matmul_mx(
                 out=warm_bank[:],
@@ -103,9 +102,9 @@ def tile_picked_haar_gelu_p_kernel(tc, x_words, x_scales, w1, w2, w3, offs, out)
         hidden = [reused.tile([P, H], F32, name="hidden0", offset=T, align_bytes=64)]
         hidden.extend(keep.tile([P, H], F32, name=f"hidden{g}") for g in range(1, GROUPS))
 
-        def first_layer(g):
+        def first_layer(g, at):
             s, first = divmod(g * GROUP, SLICE)
-            bank = hidden_psum.tile([P, PACK, GROUP], F32, name="hidden_bank")
+            bank = psum.tile([P, PACK, GROUP], F32, name=f"product{g}", tag=f"bank{at}")
             for t in range(PACK):
                 nc.tensor.matmul_mx(
                     out=bank[:, t, :],
@@ -120,11 +119,12 @@ def tile_picked_haar_gelu_p_kernel(tc, x_words, x_scales, w1, w2, w3, offs, out)
                 hidden[g][:].rearrange("p (n t) -> p n t", t=PACK), bank[:].rearrange("p t n -> p n t"), GELU
             )
 
-        def first_layer_by_rows(g, width=H):
+        def first_layer_by_rows(g, *at):
             s, first = divmod(g * GROUP, SLICE)
-            for lo in range(0, H, width):
-                cols = slice(lo, lo + width)
-                bank = hidden_psum.tile([P, width], F32, name="hidden_bank")
+            width = H // len(at)
+            for u, place in enumerate(at):
+                cols = slice(u * width, (u + 1) * width)
+                bank = psum.tile([P, width], F32, name=f"product{g}_{u}", tag=f"bank{place}")
                 nc.tensor.matmul_mx(
                     out=bank[:],
                     lhsT=picked_words[s][:, first : first + GROUP].bitcast(FP8X4),
@@ -139,16 +139,18 @@ def tile_picked_haar_gelu_p_kernel(tc, x_words, x_scales, w1, w2, w3, offs, out)
         bands = [keep.tile([P, 2, H], BF16, name=f"bands{g}", align_bytes=64) for g in range(PAIR_GROUPS)]
         turned_banks = {}
 
-        def turn(g):
+        def negate(g):
             negated = keep.tile([P, H], F32, name=f"negated{g}")
             nc.vector.tensor_scalar_mul(negated[:], hidden[PAIR_GROUPS + g][:], -1.0)
-            for b, second in enumerate((hidden[PAIR_GROUPS + g], negated)):
-                bank = band_psum.tile([P, PACK, GROUP], F32, name="band_bank")
-                for t in range(PACK):
-                    cols = slice(t * P, (t + 1) * P)
-                    nc.tensor.matmul(bank[:, t, :], hidden[g][:, cols], identity[:], start=True, stop=False, is_transpose=True)
-                    nc.tensor.matmul(bank[:, t, :], second[:, cols], identity[:], start=False, stop=True, is_transpose=True)
-                turned_banks[g, b] = bank
+            return negated
+
+        def turn(g, b, second, at):
+            bank = psum.tile([P, PACK, GROUP], F32, name=f"band{g}_{b}", tag=f"bank{at}")
+            for t in range(PACK):
+                cols = slice(t * P, (t + 1) * P)
+                nc.tensor.matmul(bank[:, t, :], hidden[g][:, cols], identity[:], start=True, stop=False, is_transpose=True)
+                nc.tensor.matmul(bank[:, t, :], second[:, cols], identity[:], start=False, stop=True, is_transpose=True)
+            turned_banks[g, b] = bank
 
         def empty_turned(g, b, copy):
             copy(bands[g][:, b, :].rearrange("p (n t) -> p n t", t=PACK), turned_banks[g, b][:].rearrange("p t n -> p n t"))
@@ -164,9 +166,13 @@ def tile_picked_haar_gelu_p_kernel(tc, x_words, x_scales, w1, w2, w3, offs, out)
             )
 
         def quantize_band_weights():
-            nc.vector.quantize_mx(
-                out=band_codes[:].bitcast(FP8X4), scales=band_scales[:], in_=band_bf16[:].rearrange("p b m j -> p (b m j)")
-            )
+            for b in range(2):
+                cols = slice(b * N, (b + 1) * N)
+                nc.vector.quantize_mx(
+                    out=band_codes[:, cols].bitcast(FP8X4),
+                    scales=band_scales[:, cols],
+                    in_=band_bf16[:, b].rearrange("p m j -> p (m j)"),
+                )
 
         def haar(g):
             nc.vector.tensor_tensor(bands[g][:, 0, :], hidden[g][:], hidden[PAIR_GROUPS + g][:], ADD)
@@ -174,20 +180,16 @@ def tile_picked_haar_gelu_p_kernel(tc, x_words, x_scales, w1, w2, w3, offs, out)
 
         quantized = {}
 
-        def quantize_bands(g, calls=((0, 2),)):
+        def quantize_bands(g):
             codes = keep.tile([P, 2, GROUP], U32, name=f"codes{g}", align_bytes=64)
             scales = keep.tile([P, 2, GROUP], U8, name=f"scales{g}", align_bytes=64)
-            for lo, hi in calls:
-                nc.vector.quantize_mx(
-                    out=codes[:, lo:hi, :].rearrange("p b n -> p (b n)").bitcast(FP8X4),
-                    scales=scales[:, lo:hi, :].rearrange("p b n -> p (b n)"),
-                    in_=bands[g][:, lo:hi, :].rearrange("p b c -> p (b c)"),
-                )
+            for b in range(2):
+                nc.vector.quantize_mx(out=codes[:, b, :].bitcast(FP8X4), scales=scales[:, b, :], in_=bands[g][:, b, :])
             quantized[g] = (codes, scales)
 
-        def second_layer(lo, hi, halve):
+        def second_layer(lo, hi, halve, at):
             width = (hi - lo) * GROUP
-            bank = hidden_psum.tile([P, width], F32, name="hidden_bank")
+            bank = psum.tile([P, width], F32, name=f"output{lo}", tag=f"bank{at}")
             for g in range(lo, hi):
                 codes, scales = quantized[g]
                 for b in range(2):
@@ -204,36 +206,40 @@ def tile_picked_haar_gelu_p_kernel(tc, x_words, x_scales, w1, w2, w3, offs, out)
             halve(result[:], bank[:], 0.5)
             nc.sync.dma_start(out[:, lo * GROUP : hi * GROUP], result[:])
 
-        def pair(g):
-            layer = first_layer_by_rows if g in TURNED else first_layer
-            layer(g)
-            layer(PAIR_GROUPS + g)
-
         round_band_weights(0, nc.scalar.copy)
-        first_layer_by_rows(0, HALF)
-        first_layer(1)
-        first_layer_by_rows(PAIR_GROUPS)
-        first_layer(PAIR_GROUPS + 1)
-        for g in (2, 3, 5, 4):
-            pair(g)
         round_band_weights(1, nc.vector.tensor_copy)
-        turn(0)
+        first_layer_by_rows(0, 0, 1)
+        first_layer(1, 2)
+        first_layer_by_rows(6, 3)
+        negated = negate(0)
+        first_layer(7, 4)
+        first_layer(2, 5)
+        first_layer(8, 6)
+        first_layer(3, 7)
+        first_layer(9, 0)
+        turn(0, 0, hidden[6], 1)
+        first_layer_by_rows(5, 2)
+        first_layer_by_rows(11, 3)
+        first_layer(4, 4)
+        turn(0, 1, negated, 5)
+        first_layer(10, 6)
+        turn(5, 0, hidden[11], 7)
+        turn(5, 1, negate(5), 0)
         quantize_band_weights()
         haar(1)
         haar(2)
         quantize_bands(1)
         haar(3)
         quantize_bands(2)
-        turn(5)
         quantize_bands(3)
         haar(4)
         for g in TURNED:
             for b in range(2):
                 empty_turned(g, b, nc.scalar.copy)
         quantize_bands(0)
-        second_layer(1, 4, nc.scalar.mul)
+        second_layer(1, 4, nc.scalar.mul, 2)
         quantize_bands(4)
-        second_layer(0, 1, nc.scalar.mul)
-        quantize_bands(5, ((0, 1), (1, 2)))
-        second_layer(4, 5, nc.scalar.mul)
-        second_layer(5, 6, nc.vector.tensor_scalar_mul)
+        second_layer(0, 1, nc.scalar.mul, 3)
+        quantize_bands(5)
+        second_layer(4, 5, nc.scalar.mul, 4)
+        second_layer(5, 6, nc.vector.tensor_scalar_mul, 6)

@@ -15,6 +15,7 @@ U8 = mybir.dt.uint8
 FP8X4 = mybir.dt.float8_e4m3fn_x4
 GELU = mybir.ActivationFunctionType.Gelu_apprx_tanh
 COPY = mybir.ActivationFunctionType.Copy
+MULT = mybir.AluOpType.mult
 ADD = mybir.AluOpType.add
 SUBTRACT = mybir.AluOpType.subtract
 
@@ -48,8 +49,8 @@ def tile_picked_haar_gelu_p_kernel(tc, x_words, x_scales, w1, w2, w3, offs, out)
         nc.vector.memset(scale_table[:, : T // 2].bitcast(I32), 0)
         nc.gpsimd.memset(scale_table[:, T // 2 :].bitcast(I32), 0)
         w1_rows = w1.rearrange("(p j) c -> p j c", j=PACK)
-        nc.sync.dma_start(offsets[:], offs)
         nc.sync.dma_start(w1_raw[:, 0:2], w1_rows[:, 0:2])
+        nc.sync.dma_start(offsets[:], offs)
         nc.sync.dma_start(scale_table[32:96:4, :].bitcast(I32), x_scales[0].bitcast(I32))
         nc.sync.dma_start(w1_raw[:, 2:4], w1_rows[:, 2:4])
         nc.sync.dma_start(word_table[:].bitcast(I32), x_words[0].rearrange("p n t -> p (n t)").bitcast(I32))
@@ -102,7 +103,7 @@ def tile_picked_haar_gelu_p_kernel(tc, x_words, x_scales, w1, w2, w3, offs, out)
         hidden = [reused.tile([P, H], F32, name="hidden0", offset=T, align_bytes=64)]
         hidden.extend(keep.tile([P, H], F32, name=f"hidden{g}") for g in range(1, GROUPS))
 
-        def first_layer(g, at):
+        def first_layer(g, at, pieces=1):
             s, first = divmod(g * GROUP, SLICE)
             bank = psum.tile([P, PACK, GROUP], F32, name=f"product{g}", tag=f"bank{at}")
             for t in range(PACK):
@@ -115,9 +116,10 @@ def tile_picked_haar_gelu_p_kernel(tc, x_words, x_scales, w1, w2, w3, offs, out)
                     start=True,
                     stop=True,
                 )
-            nc.scalar.activation(
-                hidden[g][:].rearrange("p (n t) -> p n t", t=PACK), bank[:].rearrange("p t n -> p n t"), GELU
-            )
+            woven = hidden[g][:].rearrange("p (n t) -> p n t", t=PACK)
+            for lo in range(0, GROUP, GROUP // pieces):
+                part = slice(lo, lo + GROUP // pieces)
+                nc.scalar.activation(woven[:, part], bank[:].rearrange("p t n -> p n t")[:, part], GELU)
 
         def first_layer_by_rows(g, *at):
             s, first = divmod(g * GROUP, SLICE)
@@ -152,8 +154,9 @@ def tile_picked_haar_gelu_p_kernel(tc, x_words, x_scales, w1, w2, w3, offs, out)
                 nc.tensor.matmul(bank[:, t, :], second[:, cols], identity[:], start=False, stop=True, is_transpose=True)
             turned_banks[g, b] = bank
 
-        def empty_turned(g, b, copy):
-            copy(bands[g][:, b, :].rearrange("p (n t) -> p n t", t=PACK), turned_banks[g, b][:].rearrange("p t n -> p n t"))
+        def empty_turned(g, b, copy, lo=0, hi=GROUP):
+            woven = bands[g][:, b, :].rearrange("p (n t) -> p n t", t=PACK)
+            copy(woven[:, lo:hi], turned_banks[g, b][:].rearrange("p t n -> p n t")[:, lo:hi])
 
         band_bf16 = keep.tile([P, 2, N, PACK], BF16, name="band_bf16", align_bytes=64)
         band_codes = keep.tile([P, 2 * N], U32, name="band_codes", align_bytes=64)
@@ -174,9 +177,11 @@ def tile_picked_haar_gelu_p_kernel(tc, x_words, x_scales, w1, w2, w3, offs, out)
                     in_=band_bf16[:, b].rearrange("p m j -> p (m j)"),
                 )
 
-        def haar(g):
-            nc.vector.tensor_tensor(bands[g][:, 0, :], hidden[g][:], hidden[PAIR_GROUPS + g][:], ADD)
-            nc.vector.tensor_tensor(bands[g][:, 1, :], hidden[g][:], hidden[PAIR_GROUPS + g][:], SUBTRACT)
+        def haar(g, pieces=1):
+            for lo in range(0, H, H // pieces):
+                cols = slice(lo, lo + H // pieces)
+                for b, op in enumerate((ADD, SUBTRACT)):
+                    nc.vector.tensor_tensor(bands[g][:, b, cols], hidden[g][:, cols], hidden[PAIR_GROUPS + g][:, cols], op)
 
         quantized = {}
 
@@ -207,12 +212,16 @@ def tile_picked_haar_gelu_p_kernel(tc, x_words, x_scales, w1, w2, w3, offs, out)
             nc.sync.dma_start(out[:, lo * GROUP : hi * GROUP], result[:])
 
         round_band_weights(0, nc.scalar.copy)
-        round_band_weights(1, nc.vector.tensor_copy)
+        nc.gpsimd.tensor_scalar(
+            band_bf16[:, 1], band_raw[1][:].rearrange("p j m -> p m j"), 1.0, 0.0, op0=MULT, op1=ADD
+        )
         first_layer_by_rows(0, 0, 1)
         first_layer(1, 2)
-        first_layer_by_rows(6, 3)
+        first_layer(7, 3)
+        first_layer_by_rows(6, 4)
+        quantize_band_weights()
+        haar(1)
         negated = negate(0)
-        first_layer(7, 4)
         first_layer(2, 5)
         first_layer(8, 6)
         first_layer(3, 7)
@@ -222,20 +231,19 @@ def tile_picked_haar_gelu_p_kernel(tc, x_words, x_scales, w1, w2, w3, offs, out)
         first_layer_by_rows(11, 3)
         first_layer(4, 4)
         turn(0, 1, negated, 5)
-        first_layer(10, 6)
+        first_layer(10, 6, 2)
         turn(5, 0, hidden[11], 7)
         turn(5, 1, negate(5), 0)
-        quantize_band_weights()
-        haar(1)
         haar(2)
         quantize_bands(1)
         haar(3)
         quantize_bands(2)
+        empty_turned(0, 0, nc.vector.tensor_copy, 0, GROUP // 2)
         quantize_bands(3)
-        haar(4)
-        for g in TURNED:
-            for b in range(2):
-                empty_turned(g, b, nc.scalar.copy)
+        haar(4, 2)
+        empty_turned(0, 0, nc.scalar.copy, GROUP // 2, GROUP)
+        for g, b in ((0, 1), (5, 0), (5, 1)):
+            empty_turned(g, b, nc.scalar.copy)
         quantize_bands(0)
         second_layer(1, 4, nc.scalar.mul, 2)
         quantize_bands(4)

@@ -192,7 +192,9 @@ def tile_picked_haar_gelu_p_kernel(tc, x_words, x_scales, w1, w2, w3, offs, out)
                 nc.vector.quantize_mx(out=codes[:, b, :].bitcast(FP8X4), scales=scales[:, b, :], in_=bands[g][:, b, :])
             quantized[g] = (codes, scales)
 
-        def second_layer(lo, hi, halve, at):
+        output_banks = {}
+
+        def second_layer(lo, hi, at):
             width = (hi - lo) * GROUP
             bank = psum.tile([P, width], F32, name=f"output{lo}", tag=f"bank{at}")
             for g in range(lo, hi):
@@ -207,8 +209,11 @@ def tile_picked_haar_gelu_p_kernel(tc, x_words, x_scales, w1, w2, w3, offs, out)
                         start=(b == 0),
                         stop=(b == 1),
                     )
-            result = keep.tile([P, width], F32, name=f"result{lo}")
-            halve(result[:], bank[:], 0.5)
+            output_banks[lo, hi] = bank
+
+        def store(lo, hi, halve):
+            result = keep.tile([P, (hi - lo) * GROUP], F32, name=f"result{lo}")
+            halve(result[:], output_banks[lo, hi][:], 0.5)
             nc.sync.dma_start(out[:, lo * GROUP : hi * GROUP], result[:])
 
         round_band_weights(0, nc.scalar.copy)
@@ -218,36 +223,42 @@ def tile_picked_haar_gelu_p_kernel(tc, x_words, x_scales, w1, w2, w3, offs, out)
         first_layer_by_rows(0, 0, 1)
         first_layer(1, 2)
         first_layer(7, 3)
-        first_layer_by_rows(6, 4)
+        first_layer_by_rows(6, 0)
         quantize_band_weights()
         haar(1)
         negated = negate(0)
-        first_layer(2, 5)
-        first_layer(8, 6)
-        first_layer(3, 7)
+        first_layer(2, 1)
+        first_layer(8, 2)
+        first_layer(3, 3)
         first_layer(9, 0)
-        turn(0, 0, hidden[6], 1)
+        turn(0, 0, hidden[6], 4)
         first_layer_by_rows(5, 2)
-        first_layer_by_rows(11, 3)
-        first_layer(4, 4)
+        first_layer_by_rows(11, 1)
         turn(0, 1, negated, 5)
-        first_layer(10, 6, 2)
-        turn(5, 0, hidden[11], 7)
-        turn(5, 1, negate(5), 0)
+        first_layer(4, 0)
         haar(2)
         quantize_bands(1)
+        second_layer(1, 2, 2)
+        first_layer(10, 1, 2)
+        turn(5, 0, hidden[11], 6)
         haar(3)
+        turn(5, 1, negate(5), 7)
         quantize_bands(2)
         empty_turned(0, 0, nc.vector.tensor_copy, 0, GROUP // 2)
         quantize_bands(3)
+        second_layer(2, 4, 0)
         haar(4, 2)
         empty_turned(0, 0, nc.scalar.copy, GROUP // 2, GROUP)
         for g, b in ((0, 1), (5, 0), (5, 1)):
             empty_turned(g, b, nc.scalar.copy)
+        store(1, 2, nc.scalar.mul)
+        store(2, 4, nc.scalar.mul)
         quantize_bands(0)
-        second_layer(1, 4, nc.scalar.mul, 2)
+        second_layer(0, 1, 3)
+        store(0, 1, nc.scalar.mul)
         quantize_bands(4)
-        second_layer(0, 1, nc.scalar.mul, 3)
+        second_layer(4, 5, 1)
+        store(4, 5, nc.scalar.mul)
         quantize_bands(5)
-        second_layer(4, 5, nc.scalar.mul, 4)
-        second_layer(5, 6, nc.vector.tensor_scalar_mul, 6)
+        second_layer(5, 6, 4)
+        store(5, 6, nc.vector.tensor_scalar_mul)

@@ -27,8 +27,7 @@ PAIR_GROUPS = V // GROUP
 SLICE = 512
 HALF = H // 2
 SCALAR_SHARE = 96
-WARM_PASSES = 3
-TURNED = (0, 5)
+WARM_WIDTHS = (512, 256)
 
 
 def tile_picked_haar_gelu_p_kernel(tc, x_words, x_scales, w1, w2, w3, offs, out):
@@ -43,11 +42,10 @@ def tile_picked_haar_gelu_p_kernel(tc, x_words, x_scales, w1, w2, w3, offs, out)
         scale_table = reused.tile([P, T], U8, name="scale_table", offset=0, align_bytes=64)
         word_table = keep.tile([P, T], U32, name="word_table", align_bytes=64)
         w1_raw = keep.tile([P, PACK, H], F32, name="w1_raw")
+        nc.vector.memset(scale_table[:].bitcast(I32), 0)
         warm = keep.tile([P, 2], F32, name="warm")
         nc.vector.memset(warm[:, 0:1], 0.0)
         nc.scalar.activation(warm[:, 1:2], warm[:, 0:1], GELU)
-        nc.vector.memset(scale_table[:, : T // 2].bitcast(I32), 0)
-        nc.gpsimd.memset(scale_table[:, T // 2 :].bitcast(I32), 0)
         w1_rows = w1.rearrange("(p j) c -> p j c", j=PACK)
         nc.sync.dma_start(w1_raw[:, 0:2], w1_rows[:, 0:2])
         nc.sync.dma_start(offsets[:], offs)
@@ -56,9 +54,6 @@ def tile_picked_haar_gelu_p_kernel(tc, x_words, x_scales, w1, w2, w3, offs, out)
         nc.sync.dma_start(word_table[:].bitcast(I32), x_words[0].rearrange("p n t -> p (n t)").bitcast(I32))
         w2_raw = reused.tile([P, PACK, N], F32, name="w2_raw", offset=T, align_bytes=64)
         nc.sync.dma_start(w2_raw[:], w2.rearrange("(p j) m -> p j m", j=PACK))
-
-        identity = keep.tile([P, P], F32, name="identity")
-        make_identity(nc, identity[:])
 
         picked_rows = keep.tile([P, S], U8, name="picked_rows", align_bytes=64)
         picked_scales = keep.tile([P, S], U8, name="picked_scales", align_bytes=64)
@@ -71,7 +66,7 @@ def tile_picked_haar_gelu_p_kernel(tc, x_words, x_scales, w1, w2, w3, offs, out)
         nc.sync.dma_start(w3_raw[:], w3.rearrange("(p j) m -> p j m", j=PACK))
         band_raw = [w2_raw, w3_raw]
 
-        w1_bf16 = keep.tile([P, PACK, P, PACK], BF16, name="w1_bf16", align_bytes=64)
+        w1_bf16 = reused.tile([P, PACK, P, PACK], BF16, name="w1_bf16", offset=2 * T, align_bytes=64)
         w1_codes = keep.tile([P, H], U32, name="w1_codes", align_bytes=64)
         w1_scales = keep.tile([P, H], U8, name="w1_scales", align_bytes=64)
         dealt = w1_bf16[:].rearrange("p t m j -> p m t j")
@@ -82,14 +77,17 @@ def tile_picked_haar_gelu_p_kernel(tc, x_words, x_scales, w1, w2, w3, offs, out)
             out=w1_codes[:].bitcast(FP8X4), scales=w1_scales[:], in_=w1_bf16[:].rearrange("p t m j -> p (t m j)")
         )
 
+        identity = reused.tile([P, P], F32, name="identity", offset=2 * T, align_bytes=64)
+        make_identity(nc, identity[:])
+
         warm_bank = psum.tile([P, H], F32, name="warm_bank", tag="bank7")
-        for u in range(WARM_PASSES):
+        for width in WARM_WIDTHS:
             nc.tensor.matmul_mx(
-                out=warm_bank[:],
+                out=warm_bank[:, :width],
                 lhsT=w1_codes[:, :P].bitcast(FP8X4),
                 lhsT_scale=w1_scales[:, :P],
-                rhs=w1_codes[:].bitcast(FP8X4),
-                rhs_scale=w1_scales[:],
+                rhs=w1_codes[:, :width].bitcast(FP8X4),
+                rhs_scale=w1_scales[:, :width],
                 start=True,
                 stop=True,
             )

@@ -24,9 +24,9 @@ PACK = 4
 GROUP = 128
 GROUPS = S // GROUP
 PAIR_GROUPS = V // GROUP
-SLICE = 512
+SLICES = ((0, 2), (6, 8), (2, 6), (8, 12))
 HALF = H // 2
-SCALAR_SHARE = 96
+SCALAR_SHARE = 80
 WARM_WIDTHS = (512, 256)
 
 
@@ -42,18 +42,19 @@ def tile_picked_haar_gelu_p_kernel(tc, x_words, x_scales, w1, w2, w3, offs, out)
         scale_table = reused.tile([P, T], U8, name="scale_table", offset=0, align_bytes=64)
         word_table = keep.tile([P, T], U32, name="word_table", align_bytes=64)
         w1_raw = keep.tile([P, PACK, H], F32, name="w1_raw")
-        nc.vector.memset(scale_table[:].bitcast(I32), 0)
-        warm = keep.tile([P, 2], F32, name="warm")
-        nc.vector.memset(warm[:, 0:1], 0.0)
-        nc.scalar.activation(warm[:, 1:2], warm[:, 0:1], GELU)
+        nc.vector.memset(scale_table[:, : T // 2].bitcast(I32), 0)
+        nc.gpsimd.memset(scale_table[:, T // 2 :].bitcast(I32), 0)
         w1_rows = w1.rearrange("(p j) c -> p j c", j=PACK)
         nc.sync.dma_start(w1_raw[:, 0:2], w1_rows[:, 0:2])
         nc.sync.dma_start(offsets[:], offs)
         nc.sync.dma_start(scale_table[32:96:4, :].bitcast(I32), x_scales[0].bitcast(I32))
         nc.sync.dma_start(w1_raw[:, 2:4], w1_rows[:, 2:4])
         nc.sync.dma_start(word_table[:].bitcast(I32), x_words[0].rearrange("p n t -> p (n t)").bitcast(I32))
-        w2_raw = reused.tile([P, PACK, N], F32, name="w2_raw", offset=T, align_bytes=64)
+        w2_raw = keep.tile([P, PACK, N], F32, name="w2_raw")
         nc.sync.dma_start(w2_raw[:], w2.rearrange("(p j) m -> p j m", j=PACK))
+
+        identity = keep.tile([P, P], F32, name="identity")
+        make_identity(nc, identity[:])
 
         picked_rows = keep.tile([P, S], U8, name="picked_rows", align_bytes=64)
         picked_scales = keep.tile([P, S], U8, name="picked_scales", align_bytes=64)
@@ -66,7 +67,7 @@ def tile_picked_haar_gelu_p_kernel(tc, x_words, x_scales, w1, w2, w3, offs, out)
         nc.sync.dma_start(w3_raw[:], w3.rearrange("(p j) m -> p j m", j=PACK))
         band_raw = [w2_raw, w3_raw]
 
-        w1_bf16 = reused.tile([P, PACK, P, PACK], BF16, name="w1_bf16", offset=2 * T, align_bytes=64)
+        w1_bf16 = keep.tile([P, PACK, P, PACK], BF16, name="w1_bf16", align_bytes=64)
         w1_codes = keep.tile([P, H], U32, name="w1_codes", align_bytes=64)
         w1_scales = keep.tile([P, H], U8, name="w1_scales", align_bytes=64)
         dealt = w1_bf16[:].rearrange("p t m j -> p m t j")
@@ -76,9 +77,6 @@ def tile_picked_haar_gelu_p_kernel(tc, x_words, x_scales, w1, w2, w3, offs, out)
         nc.vector.quantize_mx(
             out=w1_codes[:].bitcast(FP8X4), scales=w1_scales[:], in_=w1_bf16[:].rearrange("p t m j -> p (t m j)")
         )
-
-        identity = reused.tile([P, P], F32, name="identity", offset=2 * T, align_bytes=64)
-        make_identity(nc, identity[:])
 
         warm_bank = psum.tile([P, H], F32, name="warm_bank", tag="bank7")
         for width in WARM_WIDTHS:
@@ -92,24 +90,23 @@ def tile_picked_haar_gelu_p_kernel(tc, x_words, x_scales, w1, w2, w3, offs, out)
                 stop=True,
             )
 
-        picked_words = []
-        for s in range(S // SLICE):
-            picked = keep.tile([P, SLICE], U32, name=f"picked_words{s}", align_bytes=64)
-            nc.vector.tensor_copy(picked[:], word_table[:].indirect(offsets[:, s * SLICE // 16 : (s + 1) * SLICE // 16]))
-            picked_words.append(picked)
+        picked_words = {}
+        for lo, hi in SLICES:
+            picked = keep.tile([P, (hi - lo) * GROUP], U32, name=f"picked_words{lo}", align_bytes=64)
+            nc.vector.tensor_copy(picked[:], word_table[:].indirect(offsets[:, lo * GROUP // 16 : hi * GROUP // 16]))
+            for g in range(lo, hi):
+                picked_words.setdefault(g, picked[:, (g - lo) * GROUP : (g - lo + 1) * GROUP])
 
-        hidden = [reused.tile([P, H], F32, name="hidden0", offset=T, align_bytes=64)]
-        hidden.extend(keep.tile([P, H], F32, name=f"hidden{g}") for g in range(1, GROUPS))
+        hidden = [keep.tile([P, H], F32, name=f"hidden{g}") for g in range(GROUPS)]
 
         def first_layer(g, at, pieces=1):
-            s, first = divmod(g * GROUP, SLICE)
             bank = psum.tile([P, PACK, GROUP], F32, name=f"product{g}", tag=f"bank{at}")
             for t in range(PACK):
                 nc.tensor.matmul_mx(
                     out=bank[:, t, :],
                     lhsT=w1_codes[:, t * P : (t + 1) * P].bitcast(FP8X4),
                     lhsT_scale=w1_scales[:, t * P : (t + 1) * P],
-                    rhs=picked_words[s][:, first : first + GROUP].bitcast(FP8X4),
+                    rhs=picked_words[g].bitcast(FP8X4),
                     rhs_scale=picked_scales[:, g * GROUP : (g + 1) * GROUP],
                     start=True,
                     stop=True,
@@ -120,14 +117,13 @@ def tile_picked_haar_gelu_p_kernel(tc, x_words, x_scales, w1, w2, w3, offs, out)
                 nc.scalar.activation(woven[:, part], bank[:].rearrange("p t n -> p n t")[:, part], GELU)
 
         def first_layer_by_rows(g, *at):
-            s, first = divmod(g * GROUP, SLICE)
             width = H // len(at)
             for u, place in enumerate(at):
                 cols = slice(u * width, (u + 1) * width)
                 bank = psum.tile([P, width], F32, name=f"product{g}_{u}", tag=f"bank{place}")
                 nc.tensor.matmul_mx(
                     out=bank[:],
-                    lhsT=picked_words[s][:, first : first + GROUP].bitcast(FP8X4),
+                    lhsT=picked_words[g].bitcast(FP8X4),
                     lhsT_scale=picked_scales[:, g * GROUP : (g + 1) * GROUP],
                     rhs=w1_codes[:, cols].bitcast(FP8X4),
                     rhs_scale=w1_scales[:, cols],
@@ -160,10 +156,9 @@ def tile_picked_haar_gelu_p_kernel(tc, x_words, x_scales, w1, w2, w3, offs, out)
         band_codes = keep.tile([P, 2 * N], U32, name="band_codes", align_bytes=64)
         band_scales = keep.tile([P, 2 * N], U8, name="band_scales", align_bytes=64)
 
-        def round_band_weights(b, copy):
-            copy(
-                band_bf16[:, b].rearrange("p (c i) j -> p c j i", i=PACK),
-                band_raw[b][:].rearrange("p j (c i) -> p c j i", i=PACK),
+        def round_band_weights(b):
+            nc.gpsimd.tensor_scalar(
+                band_bf16[:, b], band_raw[b][:].rearrange("p j m -> p m j"), 1.0, 0.0, op0=MULT, op1=ADD
             )
 
         def quantize_band_weights():
@@ -214,10 +209,8 @@ def tile_picked_haar_gelu_p_kernel(tc, x_words, x_scales, w1, w2, w3, offs, out)
             halve(result[:], output_banks[lo, hi][:], 0.5)
             nc.sync.dma_start(out[:, lo * GROUP : hi * GROUP], result[:])
 
-        round_band_weights(0, nc.scalar.copy)
-        nc.gpsimd.tensor_scalar(
-            band_bf16[:, 1], band_raw[1][:].rearrange("p j m -> p m j"), 1.0, 0.0, op0=MULT, op1=ADD
-        )
+        round_band_weights(0)
+        round_band_weights(1)
         first_layer_by_rows(0, 0, 1)
         first_layer(1, 2)
         first_layer(7, 3)
@@ -242,11 +235,11 @@ def tile_picked_haar_gelu_p_kernel(tc, x_words, x_scales, w1, w2, w3, offs, out)
         haar(3)
         turn(5, 1, negate(5), 7)
         quantize_bands(2)
-        empty_turned(0, 0, nc.vector.tensor_copy, 0, GROUP // 2)
+        empty_turned(0, 0, nc.vector.tensor_copy, 0, GROUP // 4)
         quantize_bands(3)
         second_layer(2, 4, 0)
         haar(4, 2)
-        empty_turned(0, 0, nc.scalar.copy, GROUP // 2, GROUP)
+        empty_turned(0, 0, nc.scalar.copy, GROUP // 4, GROUP)
         for g, b in ((0, 1), (5, 0), (5, 1)):
             empty_turned(g, b, nc.scalar.copy)
         store(1, 2, nc.scalar.mul)

@@ -235,11 +235,11 @@ def tile_picked_haar_gelu_p_kernel(tc, x_words, x_scales, w1, w2, w3, offs, out)
         haar(3)
         turn(5, 1, negate(5), 7)
         quantize_bands(2)
-        empty_turned(0, 0, nc.vector.tensor_copy, 0, GROUP // 4)
+        empty_turned(0, 0, nc.vector.tensor_copy, 0, GROUP // 2)
         quantize_bands(3)
         second_layer(2, 4, 0)
         haar(4, 2)
-        empty_turned(0, 0, nc.scalar.copy, GROUP // 4, GROUP)
+        empty_turned(0, 0, nc.scalar.copy, GROUP // 2, GROUP)
         for g, b in ((0, 1), (5, 0), (5, 1)):
             empty_turned(g, b, nc.scalar.copy)
         store(1, 2, nc.scalar.mul)

@@ -27,7 +27,6 @@ PAIR_GROUPS = V // GROUP
 SLICES = ((0, 2), (6, 8), (2, 6), (8, 12))
 HALF = H // 2
 SCALAR_SHARE = 80
-WARM_WIDTHS = (512, 256)
 
 
 def tile_picked_haar_gelu_p_kernel(tc, x_words, x_scales, w1, w2, w3, offs, out):
@@ -77,18 +76,6 @@ def tile_picked_haar_gelu_p_kernel(tc, x_words, x_scales, w1, w2, w3, offs, out)
         nc.vector.quantize_mx(
             out=w1_codes[:].bitcast(FP8X4), scales=w1_scales[:], in_=w1_bf16[:].rearrange("p t m j -> p (t m j)")
         )
-
-        warm_bank = psum.tile([P, H], F32, name="warm_bank", tag="bank7")
-        for width in WARM_WIDTHS:
-            nc.tensor.matmul_mx(
-                out=warm_bank[:, :width],
-                lhsT=w1_codes[:, :P].bitcast(FP8X4),
-                lhsT_scale=w1_scales[:, :P],
-                rhs=w1_codes[:, :width].bitcast(FP8X4),
-                rhs_scale=w1_scales[:, :width],
-                start=True,
-                stop=True,
-            )
 
         picked_words = {}
         for lo, hi in SLICES:

@@ -14,7 +14,6 @@ U16 = mybir.dt.uint16
 U8 = mybir.dt.uint8
 FP8X4 = mybir.dt.float8_e4m3fn_x4
 GELU = mybir.ActivationFunctionType.Gelu_apprx_tanh
-COPY = mybir.ActivationFunctionType.Copy
 MULT = mybir.AluOpType.mult
 ADD = mybir.AluOpType.add
 SUBTRACT = mybir.AluOpType.subtract
@@ -23,9 +22,8 @@ P = 128
 PACK = 4
 GROUP = 128
 GROUPS = S // GROUP
-PAIR_GROUPS = V // GROUP
-SLICES = ((0, 2), (6, 8), (2, 6), (8, 12))
-HALF = H // 2
+PAIRS = V // GROUP
+SLICES = ((0, 2), (6, 8), (2, 4), (8, 12), (4, 6))
 SCALAR_SHARE = 80
 
 
@@ -35,6 +33,8 @@ def tile_picked_haar_gelu_p_kernel(tc, x_words, x_scales, w1, w2, w3, offs, out)
         lists = ctx.enter_context(tc.tile_pool(name="lists", bufs=1))
         keep = ctx.enter_context(tc.tile_pool(name="keep", bufs=1))
         reused = ctx.enter_context(tc.tile_pool(name="reused", bufs=1))
+        late = ctx.enter_context(tc.tile_pool(name="late", bufs=1))
+        early = ctx.enter_context(tc.tile_pool(name="early", bufs=1))
         psum = ctx.enter_context(tc.psum_pool(name="psum", bufs=1))
 
         offsets = lists.tile([P, S // 16], U16, name="offsets")
@@ -64,7 +64,6 @@ def tile_picked_haar_gelu_p_kernel(tc, x_words, x_scales, w1, w2, w3, offs, out)
 
         w3_raw = reused.tile([P, PACK, N], F32, name="w3_raw", offset=0, align_bytes=64)
         nc.sync.dma_start(w3_raw[:], w3.rearrange("(p j) m -> p j m", j=PACK))
-        band_raw = [w2_raw, w3_raw]
 
         w1_bf16 = keep.tile([P, PACK, P, PACK], BF16, name="w1_bf16", align_bytes=64)
         w1_codes = keep.tile([P, H], U32, name="w1_codes", align_bytes=64)
@@ -77,16 +76,41 @@ def tile_picked_haar_gelu_p_kernel(tc, x_words, x_scales, w1, w2, w3, offs, out)
             out=w1_codes[:].bitcast(FP8X4), scales=w1_scales[:], in_=w1_bf16[:].rearrange("p t m j -> p (t m j)")
         )
 
+        band_bf16 = early.tile([P, 2, N, PACK], BF16, name="band_bf16", offset=0, align_bytes=64)
+        for b, raw in enumerate((w2_raw, w3_raw)):
+            nc.gpsimd.tensor_scalar(band_bf16[:, b], raw[:].rearrange("p j m -> p m j"), 1.0, 0.0, op0=MULT, op1=ADD)
+
+        quantized = {}
+
+        def quantize(key, values, held=None, calls=2):
+            codes = keep.tile([P, 2 * GROUP], U32, name=f"codes{key}", align_bytes=64)
+            if held is None:
+                scales = keep.tile([P, 2 * GROUP], U8, name=f"scales{key}", align_bytes=64)
+            else:
+                scales = late.tile([P, 2 * GROUP], U8, name=f"scales{key}", offset=held * 2 * GROUP, align_bytes=64)
+            width = 2 * GROUP // calls
+            for lo in range(0, 2 * GROUP, width):
+                cols = slice(lo, lo + width)
+                nc.vector.quantize_mx(
+                    out=codes[:, cols].bitcast(FP8X4), scales=scales[:, cols], in_=values[:, PACK * lo : PACK * (lo + width)]
+                )
+            quantized[key] = (codes, scales)
+
         picked_words = {}
         for lo, hi in SLICES:
-            picked = keep.tile([P, (hi - lo) * GROUP], U32, name=f"picked_words{lo}", align_bytes=64)
+            if (lo, hi) == SLICES[-1]:
+                quantize("w", band_bf16[:].rearrange("p b m j -> p (b m j)"), None, 1)
+                picked = early.tile([P, (hi - lo) * GROUP], U32, name=f"picked_words{lo}", offset=0, align_bytes=64)
+            else:
+                picked = keep.tile([P, (hi - lo) * GROUP], U32, name=f"picked_words{lo}", align_bytes=64)
             nc.vector.tensor_copy(picked[:], word_table[:].indirect(offsets[:, lo * GROUP // 16 : hi * GROUP // 16]))
             for g in range(lo, hi):
                 picked_words.setdefault(g, picked[:, (g - lo) * GROUP : (g - lo + 1) * GROUP])
 
-        hidden = [keep.tile([P, H], F32, name=f"hidden{g}") for g in range(GROUPS)]
+        hidden = [keep.tile([P, H], F32, name=f"hidden{g}") for g in range(GROUPS) if g != 8]
+        hidden.insert(8, late.tile([P, H], F32, name="hidden8", offset=0, align_bytes=64))
 
-        def first_layer(g, at, pieces=1):
+        def by_channels(g, at):
             bank = psum.tile([P, PACK, GROUP], F32, name=f"product{g}", tag=f"bank{at}")
             for t in range(PACK):
                 nc.tensor.matmul_mx(
@@ -98,12 +122,11 @@ def tile_picked_haar_gelu_p_kernel(tc, x_words, x_scales, w1, w2, w3, offs, out)
                     start=True,
                     stop=True,
                 )
-            woven = hidden[g][:].rearrange("p (n t) -> p n t", t=PACK)
-            for lo in range(0, GROUP, GROUP // pieces):
-                part = slice(lo, lo + GROUP // pieces)
-                nc.scalar.activation(woven[:, part], bank[:].rearrange("p t n -> p n t")[:, part], GELU)
+            nc.scalar.activation(
+                hidden[g][:].rearrange("p (n t) -> p n t", t=PACK), bank[:].rearrange("p t n -> p n t"), GELU
+            )
 
-        def first_layer_by_rows(g, *at):
+        def by_patches(g, *at):
             width = H // len(at)
             for u, place in enumerate(at):
                 cols = slice(u * width, (u + 1) * width)
@@ -119,73 +142,53 @@ def tile_picked_haar_gelu_p_kernel(tc, x_words, x_scales, w1, w2, w3, offs, out)
                 )
                 nc.scalar.activation(hidden[g][:, cols], bank[:], GELU)
 
-        bands = [keep.tile([P, 2, H], BF16, name=f"bands{g}", align_bytes=64) for g in range(PAIR_GROUPS)]
-        turned_banks = {}
+        bands = [
+            early.tile([P, 2, H], BF16, name=f"bands{g}", offset=2 * H, align_bytes=64)
+            if g == 1
+            else keep.tile([P, 2, H], BF16, name=f"bands{g}", align_bytes=64)
+            for g in range(PAIRS)
+        ]
+        turned = {}
 
-        def negate(g):
-            negated = keep.tile([P, H], F32, name=f"negated{g}")
-            nc.vector.tensor_scalar_mul(negated[:], hidden[PAIR_GROUPS + g][:], -1.0)
-            return negated
-
-        def turn(g, b, second, at):
-            bank = psum.tile([P, PACK, GROUP], F32, name=f"band{g}_{b}", tag=f"bank{at}")
+        def turn(key, at, *terms):
+            bank = psum.tile([P, PACK, GROUP], F32, name=f"turned{key}", tag=f"bank{at}")
             for t in range(PACK):
                 cols = slice(t * P, (t + 1) * P)
-                nc.tensor.matmul(bank[:, t, :], hidden[g][:, cols], identity[:], start=True, stop=False, is_transpose=True)
-                nc.tensor.matmul(bank[:, t, :], second[:, cols], identity[:], start=False, stop=True, is_transpose=True)
-            turned_banks[g, b] = bank
+                for i, term in enumerate(terms):
+                    nc.tensor.matmul(
+                        bank[:, t, :], term[:, cols], identity[:], start=(i == 0), stop=(i == len(terms) - 1), is_transpose=True
+                    )
+            turned[key] = bank[:].rearrange("p t n -> p n t")
 
-        def empty_turned(g, b, copy, lo=0, hi=GROUP):
-            woven = bands[g][:, b, :].rearrange("p (n t) -> p n t", t=PACK)
-            copy(woven[:, lo:hi], turned_banks[g, b][:].rearrange("p t n -> p n t")[:, lo:hi])
+        def woven(ap):
+            return ap.rearrange("p (n t) -> p n t", t=PACK)
 
-        band_bf16 = keep.tile([P, 2, N, PACK], BF16, name="band_bf16", align_bytes=64)
-        band_codes = keep.tile([P, 2 * N], U32, name="band_codes", align_bytes=64)
-        band_scales = keep.tile([P, 2 * N], U8, name="band_scales", align_bytes=64)
+        def haar(g, engine):
+            for b, op in enumerate((ADD, SUBTRACT)):
+                engine.tensor_tensor(bands[g][:, b, :], hidden[g][:], hidden[PAIRS + g][:], op)
 
-        def round_band_weights(b):
-            nc.gpsimd.tensor_scalar(
-                band_bf16[:, b], band_raw[b][:].rearrange("p j m -> p m j"), 1.0, 0.0, op0=MULT, op1=ADD
-            )
+        def haar_from_psum(g):
+            for b, op in enumerate((ADD, SUBTRACT)):
+                nc.vector.tensor_tensor(woven(bands[g][:, b, :]), turned[f"first{g}"], woven(hidden[PAIRS + g][:]), op)
 
-        def quantize_band_weights():
-            for b in range(2):
-                cols = slice(b * N, (b + 1) * N)
-                nc.vector.quantize_mx(
-                    out=band_codes[:, cols].bitcast(FP8X4),
-                    scales=band_scales[:, cols],
-                    in_=band_bf16[:, b].rearrange("p m j -> p (m j)"),
-                )
-
-        def haar(g, pieces=1):
-            for lo in range(0, H, H // pieces):
-                cols = slice(lo, lo + H // pieces)
-                for b, op in enumerate((ADD, SUBTRACT)):
-                    nc.vector.tensor_tensor(bands[g][:, b, cols], hidden[g][:, cols], hidden[PAIR_GROUPS + g][:, cols], op)
-
-        quantized = {}
-
-        def quantize_bands(g):
-            codes = keep.tile([P, 2, GROUP], U32, name=f"codes{g}", align_bytes=64)
-            scales = keep.tile([P, 2, GROUP], U8, name=f"scales{g}", align_bytes=64)
-            for b in range(2):
-                nc.vector.quantize_mx(out=codes[:, b, :].bitcast(FP8X4), scales=scales[:, b, :], in_=bands[g][:, b, :])
-            quantized[g] = (codes, scales)
+        def quantize_bands(g, held=None, calls=2):
+            quantize(g, bands[g][:].rearrange("p b c -> p (b c)"), held, calls)
 
         output_banks = {}
 
         def second_layer(lo, hi, at):
-            width = (hi - lo) * GROUP
-            bank = psum.tile([P, width], F32, name=f"output{lo}", tag=f"bank{at}")
+            band_codes, band_scales = quantized["w"]
+            bank = psum.tile([P, (hi - lo) * GROUP], F32, name=f"output{lo}", tag=f"bank{at}")
             for g in range(lo, hi):
                 codes, scales = quantized[g]
                 for b in range(2):
+                    cols = slice(b * GROUP, (b + 1) * GROUP)
                     nc.tensor.matmul_mx(
                         out=bank[:, (g - lo) * GROUP : (g - lo + 1) * GROUP],
-                        lhsT=band_codes[:, b * N : (b + 1) * N].bitcast(FP8X4),
-                        lhsT_scale=band_scales[:, b * N : (b + 1) * N],
-                        rhs=codes[:, b, :].bitcast(FP8X4),
-                        rhs_scale=scales[:, b, :],
+                        lhsT=band_codes[:, cols].bitcast(FP8X4),
+                        lhsT_scale=band_scales[:, cols],
+                        rhs=codes[:, cols].bitcast(FP8X4),
+                        rhs_scale=scales[:, cols],
                         start=(b == 0),
                         stop=(b == 1),
                     )
@@ -196,47 +199,42 @@ def tile_picked_haar_gelu_p_kernel(tc, x_words, x_scales, w1, w2, w3, offs, out)
             halve(result[:], output_banks[lo, hi][:], 0.5)
             nc.sync.dma_start(out[:, lo * GROUP : hi * GROUP], result[:])
 
-        round_band_weights(0)
-        round_band_weights(1)
-        first_layer_by_rows(0, 0, 1)
-        first_layer(1, 2)
-        first_layer(7, 3)
-        first_layer_by_rows(6, 0)
-        quantize_band_weights()
-        haar(1)
-        negated = negate(0)
-        first_layer(2, 1)
-        first_layer(8, 2)
-        first_layer(3, 3)
-        first_layer(9, 0)
-        turn(0, 0, hidden[6], 4)
-        first_layer_by_rows(5, 2)
-        first_layer_by_rows(11, 1)
-        turn(0, 1, negated, 5)
-        first_layer(4, 0)
-        haar(2)
-        quantize_bands(1)
-        second_layer(1, 2, 2)
-        first_layer(10, 1, 2)
-        turn(5, 0, hidden[11], 6)
-        haar(3)
-        turn(5, 1, negate(5), 7)
-        quantize_bands(2)
-        empty_turned(0, 0, nc.vector.tensor_copy, 0, GROUP // 2)
-        quantize_bands(3)
-        second_layer(2, 4, 0)
-        haar(4, 2)
-        empty_turned(0, 0, nc.scalar.copy, GROUP // 2, GROUP)
-        for g, b in ((0, 1), (5, 0), (5, 1)):
-            empty_turned(g, b, nc.scalar.copy)
-        store(1, 2, nc.scalar.mul)
-        store(2, 4, nc.scalar.mul)
-        quantize_bands(0)
-        second_layer(0, 1, 3)
-        store(0, 1, nc.scalar.mul)
+        by_patches(0, 0, 1)
+        by_channels(1, 2)
+        by_channels(7, 3)
+        by_channels(6, 0)
+        turn("first0", 4, hidden[0])
+        haar(1, nc.gpsimd)
+        haar_from_psum(0)
+        by_patches(2, 1, 2)
+        by_channels(8, 3)
+        by_patches(9, 0)
+        turn("first2", 5, hidden[2])
+        haar_from_psum(2)
+        by_patches(3, 1)
+        negated = keep.tile([P, H], F32, name="negated")
+        nc.vector.tensor_scalar_mul(negated[:], hidden[9][:], -1.0)
+        quantize_bands(0, 1, 1)
+        quantize_bands(1, 2, 1)
+        quantize_bands(2, None, 1)
+        by_channels(4, 2)
+        by_channels(10, 3)
+        by_channels(5, 0)
+        by_channels(11, 1)
+        turn("low3", 4, hidden[3], hidden[9])
+        turn("high3", 5, hidden[3], negated)
+        second_layer(0, 3, 6)
+        haar(4, nc.vector)
+        haar(5, nc.vector)
+        nc.scalar.copy(woven(bands[3][:, 0, :]), turned["low3"])
+        nc.scalar.copy(woven(bands[3][:, 1, :]), turned["high3"])
+        store(0, 3, nc.scalar.mul)
         quantize_bands(4)
-        second_layer(4, 5, 1)
+        second_layer(4, 5, 7)
         store(4, 5, nc.scalar.mul)
+        quantize_bands(3)
+        second_layer(3, 4, 2)
+        store(3, 4, nc.scalar.mul)
         quantize_bands(5)
-        second_layer(5, 6, 4)
+        second_layer(5, 6, 3)
         store(5, 6, nc.vector.tensor_scalar_mul)

@@ -49,8 +49,6 @@ def tile_picked_haar_gelu_p_kernel(tc, x_words, x_scales, w1, w2, w3, offs, out)
         nc.sync.dma_start(scale_table[32:96:4, :].bitcast(I32), x_scales[0].bitcast(I32))
         nc.sync.dma_start(w1_raw[:, 2:4], w1_rows[:, 2:4])
         nc.sync.dma_start(word_table[:].bitcast(I32), x_words[0].rearrange("p n t -> p (n t)").bitcast(I32))
-        w2_raw = keep.tile([P, PACK, N], F32, name="w2_raw")
-        nc.sync.dma_start(w2_raw[:], w2.rearrange("(p j) m -> p j m", j=PACK))
 
         identity = keep.tile([P, P], F32, name="identity")
         make_identity(nc, identity[:])
@@ -62,6 +60,8 @@ def tile_picked_haar_gelu_p_kernel(tc, x_words, x_scales, w1, w2, w3, offs, out)
         for r in range(4):
             nc.sync.dma_start(picked_scales[r:P:32, :].bitcast(I32), picked_rows[32 + 4 * r : 96 : 16, :].bitcast(I32))
 
+        w2_raw = reused.tile([P, PACK, N], F32, name="w2_raw", offset=T // 2, align_bytes=64)
+        nc.sync.dma_start(w2_raw[:], w2.rearrange("(p j) m -> p j m", j=PACK))
         w3_raw = reused.tile([P, PACK, N], F32, name="w3_raw", offset=0, align_bytes=64)
         nc.sync.dma_start(w3_raw[:], w3.rearrange("(p j) m -> p j m", j=PACK))
 

@@ -96,6 +96,18 @@ def tile_picked_haar_gelu_p_kernel(tc, x_words, x_scales, w1, w2, w3, offs, out)
                 )
             quantized[key] = (codes, scales)
 
+        for at, width in ((6, H), (7, H // 2)):
+            unread = psum.tile([P, width], F32, name=f"unread{at}", tag=f"bank{at}")
+            nc.tensor.matmul_mx(
+                out=unread[:],
+                lhsT=w1_codes[:, :P].bitcast(FP8X4),
+                lhsT_scale=w1_scales[:, :P],
+                rhs=w1_codes[:, :width].bitcast(FP8X4),
+                rhs_scale=w1_scales[:, :width],
+                start=True,
+                stop=True,
+            )
+
         picked_words = {}
         for lo, hi in SLICES:
             if (lo, hi) == SLICES[-1]:

@@ -232,20 +232,20 @@ def tile_picked_haar_gelu_p_kernel(tc, x_words, x_scales, w1, w2, w3, offs, out)
         by_channels(4, 2)
         by_channels(10, 3)
         by_channels(5, 0)
-        by_channels(11, 1)
+        by_channels(11, 2)
         turn("low3", 4, hidden[3], hidden[9])
         turn("high3", 5, hidden[3], negated)
-        second_layer(0, 3, 6)
+        second_layer(0, 3, 0)
         haar(4, nc.vector)
+        quantize_bands(4)
+        second_layer(4, 5, 7)
         haar(5, nc.vector)
         nc.scalar.copy(woven(bands[3][:, 0, :]), turned["low3"])
         nc.scalar.copy(woven(bands[3][:, 1, :]), turned["high3"])
         store(0, 3, nc.scalar.mul)
-        quantize_bands(4)
-        second_layer(4, 5, 7)
         store(4, 5, nc.scalar.mul)
         quantize_bands(3)
-        second_layer(3, 4, 2)
+        second_layer(3, 4, 1)
         store(3, 4, nc.scalar.mul)
         quantize_bands(5)
         second_layer(5, 6, 3)

@@ -57,13 +57,21 @@ def tile_picked_haar_gelu_p_kernel(tc, x_words, x_scales, w1, w2, w3, offs, out)
         picked_scales = keep.tile([P, S], U8, name="picked_scales", align_bytes=64)
         nc.vector.memset(picked_scales[:].bitcast(I32), 0)
         nc.vector.tensor_copy(picked_rows[:], scale_table[:].indirect(offsets[:]))
-        for r in range(4):
-            nc.sync.dma_start(picked_scales[r:P:32, :].bitcast(I32), picked_rows[32 + 4 * r : 96 : 16, :].bitcast(I32))
+
+        def move_scales(cols):
+            for r in range(4):
+                nc.sync.dma_start(
+                    picked_scales[r:P:32, :].bitcast(I32).rearrange("p (d v) -> p d v", d=2)[:, :, cols],
+                    picked_rows[32 + 4 * r : 96 : 16, :].bitcast(I32).rearrange("p (d v) -> p d v", d=2)[:, :, cols],
+                )
+
+        move_scales(slice(0, 2 * GROUP // 4))
 
         w2_raw = reused.tile([P, PACK, N], F32, name="w2_raw", offset=T // 2, align_bytes=64)
         nc.sync.dma_start(w2_raw[:], w2.rearrange("(p j) m -> p j m", j=PACK))
         w3_raw = reused.tile([P, PACK, N], F32, name="w3_raw", offset=0, align_bytes=64)
         nc.sync.dma_start(w3_raw[:], w3.rearrange("(p j) m -> p j m", j=PACK))
+        move_scales(slice(2 * GROUP // 4, V // 4))
 
         w1_bf16 = keep.tile([P, PACK, P, PACK], BF16, name="w1_bf16", align_bytes=64)
         w1_codes = keep.tile([P, H], U32, name="w1_codes", align_bytes=64)

@@ -41,8 +41,7 @@ def tile_picked_haar_gelu_p_kernel(tc, x_words, x_scales, w1, w2, w3, offs, out)
         scale_table = reused.tile([P, T], U8, name="scale_table", offset=0, align_bytes=64)
         word_table = keep.tile([P, T], U32, name="word_table", align_bytes=64)
         w1_raw = keep.tile([P, PACK, H], F32, name="w1_raw")
-        nc.vector.memset(scale_table[:, : T // 2].bitcast(I32), 0)
-        nc.gpsimd.memset(scale_table[:, T // 2 :].bitcast(I32), 0)
+        nc.vector.memset(scale_table[:].bitcast(I32), 0)
         w1_rows = w1.rearrange("(p j) c -> p j c", j=PACK)
         nc.sync.dma_start(w1_raw[:, 0:2], w1_rows[:, 0:2])
         nc.sync.dma_start(offsets[:], offs)
@@ -51,7 +50,8 @@ def tile_picked_haar_gelu_p_kernel(tc, x_words, x_scales, w1, w2, w3, offs, out)
         nc.sync.dma_start(word_table[:].bitcast(I32), x_words[0].rearrange("p n t -> p (n t)").bitcast(I32))
 
         identity = keep.tile([P, P], F32, name="identity")
-        make_identity(nc, identity[:])
+        nc.vector.memset(identity[:], 0.0)
+        make_identity(nc, identity[:], nomemset=True)
 
         picked_rows = keep.tile([P, S], U8, name="picked_rows", align_bytes=64)
         picked_scales = keep.tile([P, S], U8, name="picked_scales", align_bytes=64)

@@ -24,7 +24,7 @@ GROUP = 128
 GROUPS = S // GROUP
 PAIRS = V // GROUP
 SLICES = ((0, 2), (6, 8), (2, 4), (8, 12), (4, 6))
-SCALAR_SHARE = 80
+SCALAR_SHARE = 56
 
 
 def tile_picked_haar_gelu_p_kernel(tc, x_words, x_scales, w1, w2, w3, offs, out):

@@ -38,9 +38,9 @@ def tile_picked_haar_gelu_p_kernel(tc, x_words, x_scales, w1, w2, w3, offs, out)
         psum = ctx.enter_context(tc.psum_pool(name="psum", bufs=1))
 
         offsets = lists.tile([P, S // 16], U16, name="offsets")
-        scale_table = reused.tile([P, T], U8, name="scale_table", offset=0, align_bytes=64)
-        word_table = keep.tile([P, T], U32, name="word_table", align_bytes=64)
-        w1_raw = keep.tile([P, PACK, H], F32, name="w1_raw")
+        scale_table = reused.tile([P, T], U8, name="scale_table", offset=0, align_bytes=256)
+        word_table = keep.tile([P, T], U32, name="word_table", align_bytes=256)
+        w1_raw = keep.tile([P, PACK, H], F32, name="w1_raw", align_bytes=256)
         nc.vector.memset(scale_table[:].bitcast(I32), 0)
         w1_rows = w1.rearrange("(p j) c -> p j c", j=PACK)
         nc.sync.dma_start(w1_raw[:, 0:2], w1_rows[:, 0:2])
@@ -67,9 +67,9 @@ def tile_picked_haar_gelu_p_kernel(tc, x_words, x_scales, w1, w2, w3, offs, out)
 
         move_scales(slice(0, 2 * GROUP // 4))
 
-        w2_raw = reused.tile([P, PACK, N], F32, name="w2_raw", offset=T // 2, align_bytes=64)
+        w2_raw = reused.tile([P, PACK, N], F32, name="w2_raw", offset=T // 2, align_bytes=256)
         nc.sync.dma_start(w2_raw[:], w2.rearrange("(p j) m -> p j m", j=PACK))
-        w3_raw = reused.tile([P, PACK, N], F32, name="w3_raw", offset=0, align_bytes=64)
+        w3_raw = reused.tile([P, PACK, N], F32, name="w3_raw", offset=0, align_bytes=256)
         nc.sync.dma_start(w3_raw[:], w3.rearrange("(p j) m -> p j m", j=PACK))
         move_scales(slice(2 * GROUP // 4, V // 4))
 
@@ -215,7 +215,7 @@ def tile_picked_haar_gelu_p_kernel(tc, x_words, x_scales, w1, w2, w3, offs, out)
             output_banks[lo, hi] = bank
 
         def store(lo, hi, halve):
-            result = keep.tile([P, (hi - lo) * GROUP], F32, name=f"result{lo}")
+            result = keep.tile([P, (hi - lo) * GROUP], F32, name=f"result{lo}", align_bytes=256)
             halve(result[:], output_banks[lo, hi][:], 0.5)
             nc.sync.dma_start(out[:, lo * GROUP : hi * GROUP], result[:])
 

@@ -35,6 +35,7 @@ def tile_picked_haar_gelu_p_kernel(tc, x_words, x_scales, w1, w2, w3, offs, out)
         reused = ctx.enter_context(tc.tile_pool(name="reused", bufs=1))
         late = ctx.enter_context(tc.tile_pool(name="late", bufs=1))
         early = ctx.enter_context(tc.tile_pool(name="early", bufs=1))
+        last = ctx.enter_context(tc.tile_pool(name="last", bufs=1))
         psum = ctx.enter_context(tc.psum_pool(name="psum", bufs=1))
 
         offsets = lists.tile([P, S // 16], U16, name="offsets")
@@ -121,6 +122,8 @@ def tile_picked_haar_gelu_p_kernel(tc, x_words, x_scales, w1, w2, w3, offs, out)
             if (lo, hi) == SLICES[-1]:
                 quantize("w", band_bf16[:].rearrange("p b m j -> p (b m j)"), None, 1)
                 picked = early.tile([P, (hi - lo) * GROUP], U32, name=f"picked_words{lo}", offset=0, align_bytes=64)
+            elif hi == GROUPS:
+                picked = last.tile([P, (hi - lo) * GROUP], U32, name=f"picked_words{lo}", offset=0, align_bytes=64)
             else:
                 picked = keep.tile([P, (hi - lo) * GROUP], U32, name=f"picked_words{lo}", align_bytes=64)
             nc.vector.tensor_copy(picked[:], word_table[:].indirect(offsets[:, lo * GROUP // 16 : hi * GROUP // 16]))
@@ -130,7 +133,7 @@ def tile_picked_haar_gelu_p_kernel(tc, x_words, x_scales, w1, w2, w3, offs, out)
         hidden = [keep.tile([P, H], F32, name=f"hidden{g}") for g in range(GROUPS) if g != 8]
         hidden.insert(8, late.tile([P, H], F32, name="hidden8", offset=0, align_bytes=64))
 
-        def by_channels(g, at):
+        def by_channels(g, at, between=None):
             bank = psum.tile([P, PACK, GROUP], F32, name=f"product{g}", tag=f"bank{at}")
             for t in range(PACK):
                 nc.tensor.matmul_mx(
@@ -142,6 +145,8 @@ def tile_picked_haar_gelu_p_kernel(tc, x_words, x_scales, w1, w2, w3, offs, out)
                     start=True,
                     stop=True,
                 )
+            if between:
+                between()
             nc.scalar.activation(
                 hidden[g][:].rearrange("p (n t) -> p n t", t=PACK), bank[:].rearrange("p t n -> p n t"), GELU
             )
@@ -173,12 +178,14 @@ def tile_picked_haar_gelu_p_kernel(tc, x_words, x_scales, w1, w2, w3, offs, out)
         def turn(key, at, *terms):
             bank = psum.tile([P, PACK, GROUP], F32, name=f"turned{key}", tag=f"bank{at}")
             for t in range(PACK):
-                cols = slice(t * P, (t + 1) * P)
                 for i, term in enumerate(terms):
                     nc.tensor.matmul(
-                        bank[:, t, :], term[:, cols], identity[:], start=(i == 0), stop=(i == len(terms) - 1), is_transpose=True
+                        bank[:, t, :], term(t), identity[:], start=(i == 0), stop=(i == len(terms) - 1), is_transpose=True
                     )
             turned[key] = bank[:].rearrange("p t n -> p n t")
+
+        def slots(g):
+            return lambda t: hidden[g][:, t * P : (t + 1) * P]
 
         def woven(ap):
             return ap.rearrange("p (n t) -> p n t", t=PACK)
@@ -223,26 +230,31 @@ def tile_picked_haar_gelu_p_kernel(tc, x_words, x_scales, w1, w2, w3, offs, out)
         by_channels(1, 2)
         by_channels(7, 3)
         by_channels(6, 0)
-        turn("first0", 4, hidden[0])
+        turn("first0", 4, slots(0))
         haar(1, nc.gpsimd)
         haar_from_psum(0)
         by_patches(2, 1, 2)
         by_channels(8, 3)
         by_patches(9, 0)
-        turn("first2", 5, hidden[2])
+        turn("first2", 5, slots(2))
         haar_from_psum(2)
         by_patches(3, 1)
-        negated = keep.tile([P, H], F32, name="negated")
-        nc.vector.tensor_scalar_mul(negated[:], hidden[9][:], -1.0)
+        negated = [keep.tile([P, H // 2], F32, name="negated0")]
+        nc.vector.tensor_scalar_mul(negated[0][:], hidden[9][:, : H // 2], -1.0)
         quantize_bands(0, 1, 1)
         quantize_bands(1, 2, 1)
         quantize_bands(2, None, 1)
         by_channels(4, 2)
         by_channels(10, 3)
         by_channels(5, 0)
-        by_channels(11, 2)
-        turn("low3", 4, hidden[3], hidden[9])
-        turn("high3", 5, hidden[3], negated)
+
+        def negate_rest():
+            negated.append(last.tile([P, H // 2], F32, name="negated1", offset=0, align_bytes=64))
+            nc.scalar.mul(negated[1][:], hidden[9][:, H // 2 :], -1.0)
+
+        by_channels(11, 2, negate_rest)
+        turn("low3", 4, slots(3), slots(9))
+        turn("high3", 5, slots(3), lambda t: negated[t // 2][:, (t % 2) * P : (t % 2 + 1) * P])
         second_layer(0, 3, 0)
         haar(4, nc.vector)
         quantize_bands(4)

@@ -133,7 +133,9 @@ def tile_picked_haar_gelu_p_kernel(tc, x_words, x_scales, w1, w2, w3, offs, out)
         hidden = [keep.tile([P, H], F32, name=f"hidden{g}") for g in range(GROUPS) if g != 8]
         hidden.insert(8, late.tile([P, H], F32, name="hidden8", offset=0, align_bytes=64))
 
-        def by_channels(g, at, between=None):
+        products = {}
+
+        def product_by_channels(g, at):
             bank = psum.tile([P, PACK, GROUP], F32, name=f"product{g}", tag=f"bank{at}")
             for t in range(PACK):
                 nc.tensor.matmul_mx(
@@ -145,11 +147,16 @@ def tile_picked_haar_gelu_p_kernel(tc, x_words, x_scales, w1, w2, w3, offs, out)
                     start=True,
                     stop=True,
                 )
-            if between:
-                between()
+            products[g] = bank
+
+        def gelu_by_channels(g):
             nc.scalar.activation(
-                hidden[g][:].rearrange("p (n t) -> p n t", t=PACK), bank[:].rearrange("p t n -> p n t"), GELU
+                hidden[g][:].rearrange("p (n t) -> p n t", t=PACK), products[g][:].rearrange("p t n -> p n t"), GELU
             )
+
+        def by_channels(g, at):
+            product_by_channels(g, at)
+            gelu_by_channels(g)
 
         def by_patches(g, *at):
             width = H // len(at)
@@ -246,13 +253,12 @@ def tile_picked_haar_gelu_p_kernel(tc, x_words, x_scales, w1, w2, w3, offs, out)
         quantize_bands(2, None, 1)
         by_channels(4, 2)
         by_channels(10, 3)
-        by_channels(5, 0)
-
-        def negate_rest():
-            negated.append(last.tile([P, H // 2], F32, name="negated1", offset=0, align_bytes=64))
-            nc.scalar.mul(negated[1][:], hidden[9][:, H // 2 :], -1.0)
-
-        by_channels(11, 2, negate_rest)
+        product_by_channels(5, 0)
+        product_by_channels(11, 2)
+        negated.append(last.tile([P, H // 2], F32, name="negated1", offset=0, align_bytes=64))
+        nc.scalar.mul(negated[1][:], hidden[9][:, H // 2 :], -1.0)
+        gelu_by_channels(5)
+        gelu_by_channels(11)
         turn("low3", 4, slots(3), slots(9))
         turn("high3", 5, slots(3), lambda t: negated[t // 2][:, (t % 2) * P : (t % 2 + 1) * P])
         second_layer(0, 3, 0)

@@ -50,12 +50,12 @@ def tile_picked_haar_gelu_p_kernel(tc, x_words, x_scales, w1, w2, w3, offs, out)
         nc.sync.dma_start(w1_raw[:, 2:4], w1_rows[:, 2:4])
         nc.sync.dma_start(word_table[:].bitcast(I32), x_words[0].rearrange("p n t -> p (n t)").bitcast(I32))
 
-        identity = keep.tile([P, P], F32, name="identity")
+        identity = keep.tile([P, P], F32, name="identity", align_bytes=256)
         nc.vector.memset(identity[:], 0.0)
         make_identity(nc, identity[:], nomemset=True)
 
-        picked_rows = keep.tile([P, S], U8, name="picked_rows", align_bytes=64)
-        picked_scales = keep.tile([P, S], U8, name="picked_scales", align_bytes=64)
+        picked_rows = keep.tile([P, S], U8, name="picked_rows", align_bytes=256)
+        picked_scales = keep.tile([P, S], U8, name="picked_scales", align_bytes=256)
         nc.vector.memset(picked_scales[:].bitcast(I32), 0)
         nc.vector.tensor_copy(picked_rows[:], scale_table[:].indirect(offsets[:]))
 
@@ -74,9 +74,9 @@ def tile_picked_haar_gelu_p_kernel(tc, x_words, x_scales, w1, w2, w3, offs, out)
         nc.sync.dma_start(w3_raw[:], w3.rearrange("(p j) m -> p j m", j=PACK))
         move_scales(slice(2 * GROUP // 4, V // 4))
 
-        w1_bf16 = keep.tile([P, PACK, P, PACK], BF16, name="w1_bf16", align_bytes=64)
-        w1_codes = keep.tile([P, H], U32, name="w1_codes", align_bytes=64)
-        w1_scales = keep.tile([P, H], U8, name="w1_scales", align_bytes=64)
+        w1_bf16 = keep.tile([P, PACK, P, PACK], BF16, name="w1_bf16", align_bytes=256)
+        w1_codes = keep.tile([P, H], U32, name="w1_codes", align_bytes=256)
+        w1_scales = keep.tile([P, H], U8, name="w1_scales", align_bytes=256)
         dealt = w1_bf16[:].rearrange("p t m j -> p m t j")
         rows = w1_raw[:].rearrange("p j (m t) -> p m t j", t=PACK)
         nc.scalar.copy(dealt[:, :SCALAR_SHARE], rows[:, :SCALAR_SHARE])
@@ -85,18 +85,18 @@ def tile_picked_haar_gelu_p_kernel(tc, x_words, x_scales, w1, w2, w3, offs, out)
             out=w1_codes[:].bitcast(FP8X4), scales=w1_scales[:], in_=w1_bf16[:].rearrange("p t m j -> p (t m j)")
         )
 
-        band_bf16 = early.tile([P, 2, N, PACK], BF16, name="band_bf16", offset=0, align_bytes=64)
+        band_bf16 = early.tile([P, 2, N, PACK], BF16, name="band_bf16", offset=0, align_bytes=256)
         for b, raw in enumerate((w2_raw, w3_raw)):
             nc.gpsimd.tensor_scalar(band_bf16[:, b], raw[:].rearrange("p j m -> p m j"), 1.0, 0.0, op0=MULT, op1=ADD)
 
         quantized = {}
 
         def quantize(key, values, held=None, calls=2):
-            codes = keep.tile([P, 2 * GROUP], U32, name=f"codes{key}", align_bytes=64)
+            codes = keep.tile([P, 2 * GROUP], U32, name=f"codes{key}", align_bytes=256)
             if held is None:
-                scales = keep.tile([P, 2 * GROUP], U8, name=f"scales{key}", align_bytes=64)
+                scales = keep.tile([P, 2 * GROUP], U8, name=f"scales{key}", align_bytes=256)
             else:
-                scales = late.tile([P, 2 * GROUP], U8, name=f"scales{key}", offset=held * 2 * GROUP, align_bytes=64)
+                scales = late.tile([P, 2 * GROUP], U8, name=f"scales{key}", offset=held * 2 * GROUP, align_bytes=256)
             width = 2 * GROUP // calls
             for lo in range(0, 2 * GROUP, width):
                 cols = slice(lo, lo + width)
@@ -121,17 +121,17 @@ def tile_picked_haar_gelu_p_kernel(tc, x_words, x_scales, w1, w2, w3, offs, out)
         for lo, hi in SLICES:
             if (lo, hi) == SLICES[-1]:
                 quantize("w", band_bf16[:].rearrange("p b m j -> p (b m j)"), None, 1)
-                picked = early.tile([P, (hi - lo) * GROUP], U32, name=f"picked_words{lo}", offset=0, align_bytes=64)
+                picked = early.tile([P, (hi - lo) * GROUP], U32, name=f"picked_words{lo}", offset=0, align_bytes=256)
             elif hi == GROUPS:
-                picked = last.tile([P, (hi - lo) * GROUP], U32, name=f"picked_words{lo}", offset=0, align_bytes=64)
+                picked = last.tile([P, (hi - lo) * GROUP], U32, name=f"picked_words{lo}", offset=0, align_bytes=256)
             else:
-                picked = keep.tile([P, (hi - lo) * GROUP], U32, name=f"picked_words{lo}", align_bytes=64)
+                picked = keep.tile([P, (hi - lo) * GROUP], U32, name=f"picked_words{lo}", align_bytes=256)
             nc.vector.tensor_copy(picked[:], word_table[:].indirect(offsets[:, lo * GROUP // 16 : hi * GROUP // 16]))
             for g in range(lo, hi):
                 picked_words.setdefault(g, picked[:, (g - lo) * GROUP : (g - lo + 1) * GROUP])
 
-        hidden = [keep.tile([P, H], F32, name=f"hidden{g}") for g in range(GROUPS) if g != 8]
-        hidden.insert(8, late.tile([P, H], F32, name="hidden8", offset=0, align_bytes=64))
+        hidden = [keep.tile([P, H], F32, name=f"hidden{g}", align_bytes=256) for g in range(GROUPS) if g != 8]
+        hidden.insert(8, late.tile([P, H], F32, name="hidden8", offset=0, align_bytes=256))
 
         products = {}
 
@@ -175,9 +175,9 @@ def tile_picked_haar_gelu_p_kernel(tc, x_words, x_scales, w1, w2, w3, offs, out)
                 nc.scalar.activation(hidden[g][:, cols], bank[:], GELU)
 
         bands = [
-            early.tile([P, 2, H], BF16, name=f"bands{g}", offset=2 * H, align_bytes=64)
+            early.tile([P, 2, H], BF16, name=f"bands{g}", offset=2 * H, align_bytes=256)
             if g == 1
-            else keep.tile([P, 2, H], BF16, name=f"bands{g}", align_bytes=64)
+            else keep.tile([P, 2, H], BF16, name=f"bands{g}", align_bytes=256)
             for g in range(PAIRS)
         ]
         turned = {}
@@ -246,7 +246,7 @@ def tile_picked_haar_gelu_p_kernel(tc, x_words, x_scales, w1, w2, w3, offs, out)
         turn("first2", 5, slots(2))
         haar_from_psum(2)
         by_patches(3, 1)
-        negated = [keep.tile([P, H // 2], F32, name="negated0")]
+        negated = [keep.tile([P, H // 2], F32, name="negated0", align_bytes=256)]
         nc.vector.tensor_scalar_mul(negated[0][:], hidden[9][:, : H // 2], -1.0)
         quantize_bands(0, 1, 1)
         quantize_bands(1, 2, 1)
@@ -255,7 +255,7 @@ def tile_picked_haar_gelu_p_kernel(tc, x_words, x_scales, w1, w2, w3, offs, out)
         by_channels(10, 3)
         product_by_channels(5, 0)
         product_by_channels(11, 2)
-        negated.append(last.tile([P, H // 2], F32, name="negated1", offset=0, align_bytes=64))
+        negated.append(last.tile([P, H // 2], F32, name="negated1", offset=0, align_bytes=256))
         nc.scalar.mul(negated[1][:], hidden[9][:, H // 2 :], -1.0)
         gelu_by_channels(5)
         gelu_by_channels(11)

from contextlib import ExitStack

import concourse.mybir as mybir
from concourse.masks import make_identity

K, T, S, V, H, N = 512, 4096, 1536, 768, 512, 128
FLOPS = 2 * K * H * S + 2 * 2 * H * N * V

F32 = mybir.dt.float32
BF16 = mybir.dt.bfloat16
I32 = mybir.dt.int32
U32 = mybir.dt.uint32
U16 = mybir.dt.uint16
U8 = mybir.dt.uint8
FP8X4 = mybir.dt.float8_e4m3fn_x4
GELU = mybir.ActivationFunctionType.Gelu_apprx_tanh
MULT = mybir.AluOpType.mult
ADD = mybir.AluOpType.add
SUBTRACT = mybir.AluOpType.subtract

P = 128
PACK = 4
GROUP = 128
GROUPS = S // GROUP
PAIRS = V // GROUP
SLICES = ((0, 2), (6, 8), (2, 4), (8, 12), (4, 6))
SCALAR_SHARE = 56


def tile_picked_haar_gelu_p_kernel(tc, x_words, x_scales, w1, w2, w3, offs, out):
    nc = tc.nc
    with ExitStack() as ctx:
        lists = ctx.enter_context(tc.tile_pool(name="lists", bufs=1))
        keep = ctx.enter_context(tc.tile_pool(name="keep", bufs=1))
        reused = ctx.enter_context(tc.tile_pool(name="reused", bufs=1))
        late = ctx.enter_context(tc.tile_pool(name="late", bufs=1))
        early = ctx.enter_context(tc.tile_pool(name="early", bufs=1))
        last = ctx.enter_context(tc.tile_pool(name="last", bufs=1))
        psum = ctx.enter_context(tc.psum_pool(name="psum", bufs=1))

        offsets = lists.tile([P, S // 16], U16, name="offsets")
        scale_table = reused.tile([P, T], U8, name="scale_table", offset=0, align_bytes=256)
        word_table = keep.tile([P, T], U32, name="word_table", align_bytes=256)
        w1_raw = keep.tile([P, PACK, H], F32, name="w1_raw", align_bytes=256)
        nc.vector.memset(scale_table[:].bitcast(I32), 0)
        w1_rows = w1.rearrange("(p j) c -> p j c", j=PACK)
        nc.sync.dma_start(w1_raw[:, 0:2], w1_rows[:, 0:2])
        nc.sync.dma_start(offsets[:], offs)
        nc.sync.dma_start(scale_table[32:96:4, :].bitcast(I32), x_scales[0].bitcast(I32))
        nc.sync.dma_start(w1_raw[:, 2:4], w1_rows[:, 2:4])
        nc.sync.dma_start(word_table[:].bitcast(I32), x_words[0].rearrange("p n t -> p (n t)").bitcast(I32))

        identity = keep.tile([P, P], F32, name="identity", align_bytes=256)
        nc.vector.memset(identity[:], 0.0)
        make_identity(nc, identity[:], nomemset=True)

        picked_rows = keep.tile([P, S], U8, name="picked_rows", align_bytes=256)
        picked_scales = keep.tile([P, S], U8, name="picked_scales", align_bytes=256)
        nc.vector.memset(picked_scales[:].bitcast(I32), 0)
        nc.vector.tensor_copy(picked_rows[:], scale_table[:].indirect(offsets[:]))

        def move_scales(cols):
            for r in range(4):
                nc.sync.dma_start(
                    picked_scales[r:P:32, :].bitcast(I32).rearrange("p (d v) -> p d v", d=2)[:, :, cols],
                    picked_rows[32 + 4 * r : 96 : 16, :].bitcast(I32).rearrange("p (d v) -> p d v", d=2)[:, :, cols],
                )

        move_scales(slice(0, 2 * GROUP // 4))

        w2_raw = reused.tile([P, PACK, N], F32, name="w2_raw", offset=T // 2, align_bytes=256)
        nc.sync.dma_start(w2_raw[:], w2.rearrange("(p j) m -> p j m", j=PACK))
        w3_raw = reused.tile([P, PACK, N], F32, name="w3_raw", offset=0, align_bytes=256)
        nc.sync.dma_start(w3_raw[:], w3.rearrange("(p j) m -> p j m", j=PACK))
        move_scales(slice(2 * GROUP // 4, V // 4))

        w1_bf16 = keep.tile([P, PACK, P, PACK], BF16, name="w1_bf16", align_bytes=256)
        w1_codes = keep.tile([P, H], U32, name="w1_codes", align_bytes=256)
        w1_scales = keep.tile([P, H], U8, name="w1_scales", align_bytes=256)
        dealt = w1_bf16[:].rearrange("p t m j -> p m t j")
        rows = w1_raw[:].rearrange("p j (m t) -> p m t j", t=PACK)
        nc.scalar.copy(dealt[:, :SCALAR_SHARE], rows[:, :SCALAR_SHARE])
        nc.vector.tensor_copy(dealt[:, SCALAR_SHARE:], rows[:, SCALAR_SHARE:])
        nc.vector.quantize_mx(
            out=w1_codes[:].bitcast(FP8X4), scales=w1_scales[:], in_=w1_bf16[:].rearrange("p t m j -> p (t m j)")
        )

        band_bf16 = early.tile([P, 2, N, PACK], BF16, name="band_bf16", offset=0, align_bytes=256)
        for b, raw in enumerate((w2_raw, w3_raw)):
            nc.gpsimd.tensor_scalar(band_bf16[:, b], raw[:].rearrange("p j m -> p m j"), 1.0, 0.0, op0=MULT, op1=ADD)

        quantized = {}

        def quantize(key, values, held=None, calls=2):
            codes = keep.tile([P, 2 * GROUP], U32, name=f"codes{key}", align_bytes=256)
            if held is None:
                scales = keep.tile([P, 2 * GROUP], U8, name=f"scales{key}", align_bytes=256)
            else:
                scales = late.tile([P, 2 * GROUP], U8, name=f"scales{key}", offset=held * 2 * GROUP, align_bytes=256)
            width = 2 * GROUP // calls
            for lo in range(0, 2 * GROUP, width):
                cols = slice(lo, lo + width)
                nc.vector.quantize_mx(
                    out=codes[:, cols].bitcast(FP8X4), scales=scales[:, cols], in_=values[:, PACK * lo : PACK * (lo + width)]
                )
            quantized[key] = (codes, scales)

        for at, width in ((6, H), (7, H // 2)):
            unread = psum.tile([P, width], F32, name=f"unread{at}", tag=f"bank{at}")
            nc.tensor.matmul_mx(
                out=unread[:],
                lhsT=w1_codes[:, :P].bitcast(FP8X4),
                lhsT_scale=w1_scales[:, :P],
                rhs=w1_codes[:, :width].bitcast(FP8X4),
                rhs_scale=w1_scales[:, :width],
                start=True,
                stop=True,
            )

        picked_words = {}
        for lo, hi in SLICES:
            if (lo, hi) == SLICES[-1]:
                quantize("w", band_bf16[:].rearrange("p b m j -> p (b m j)"), None, 1)
                picked = early.tile([P, (hi - lo) * GROUP], U32, name=f"picked_words{lo}", offset=0, align_bytes=256)
            elif hi == GROUPS:
                picked = last.tile([P, (hi - lo) * GROUP], U32, name=f"picked_words{lo}", offset=0, align_bytes=256)
            else:
                picked = keep.tile([P, (hi - lo) * GROUP], U32, name=f"picked_words{lo}", align_bytes=256)
            nc.vector.tensor_copy(picked[:], word_table[:].indirect(offsets[:, lo * GROUP // 16 : hi * GROUP // 16]))
            for g in range(lo, hi):
                picked_words.setdefault(g, picked[:, (g - lo) * GROUP : (g - lo + 1) * GROUP])

        hidden = [keep.tile([P, H], F32, name=f"hidden{g}", align_bytes=256) for g in range(GROUPS) if g != 8]
        hidden.insert(8, late.tile([P, H], F32, name="hidden8", offset=0, align_bytes=256))

        products = {}

        def product_by_channels(g, at):
            bank = psum.tile([P, PACK, GROUP], F32, name=f"product{g}", tag=f"bank{at}")
            for t in range(PACK):
                nc.tensor.matmul_mx(
                    out=bank[:, t, :],
                    lhsT=w1_codes[:, t * P : (t + 1) * P].bitcast(FP8X4),
                    lhsT_scale=w1_scales[:, t * P : (t + 1) * P],
                    rhs=picked_words[g].bitcast(FP8X4),
                    rhs_scale=picked_scales[:, g * GROUP : (g + 1) * GROUP],
                    start=True,
                    stop=True,
                )
            products[g] = bank

        def gelu_by_channels(g):
            nc.scalar.activation(
                hidden[g][:].rearrange("p (n t) -> p n t", t=PACK), products[g][:].rearrange("p t n -> p n t"), GELU
            )

        def by_channels(g, at):
            product_by_channels(g, at)
            gelu_by_channels(g)

        def by_patches(g, *at):
            width = H // len(at)
            for u, place in enumerate(at):
                cols = slice(u * width, (u + 1) * width)
                bank = psum.tile([P, width], F32, name=f"product{g}_{u}", tag=f"bank{place}")
                nc.tensor.matmul_mx(
                    out=bank[:],
                    lhsT=picked_words[g].bitcast(FP8X4),
                    lhsT_scale=picked_scales[:, g * GROUP : (g + 1) * GROUP],
                    rhs=w1_codes[:, cols].bitcast(FP8X4),
                    rhs_scale=w1_scales[:, cols],
                    start=True,
                    stop=True,
                )
                nc.scalar.activation(hidden[g][:, cols], bank[:], GELU)

        bands = [
            early.tile([P, 2, H], BF16, name=f"bands{g}", offset=2 * H, align_bytes=256)
            if g == 1
            else keep.tile([P, 2, H], BF16, name=f"bands{g}", align_bytes=256)
            for g in range(PAIRS)
        ]
        turned = {}

        def turn(key, at, *terms):
            bank = psum.tile([P, PACK, GROUP], F32, name=f"turned{key}", tag=f"bank{at}")
            for t in range(PACK):
                for i, term in enumerate(terms):
                    nc.tensor.matmul(
                        bank[:, t, :], term(t), identity[:], start=(i == 0), stop=(i == len(terms) - 1), is_transpose=True
                    )
            turned[key] = bank[:].rearrange("p t n -> p n t")

        def slots(g):
            return lambda t: hidden[g][:, t * P : (t + 1) * P]

        def woven(ap):
            return ap.rearrange("p (n t) -> p n t", t=PACK)

        def haar(g, engine):
            for b, op in enumerate((ADD, SUBTRACT)):
                engine.tensor_tensor(bands[g][:, b, :], hidden[g][:], hidden[PAIRS + g][:], op)

        def haar_from_psum(g):
            for b, op in enumerate((ADD, SUBTRACT)):
                nc.vector.tensor_tensor(woven(bands[g][:, b, :]), turned[f"first{g}"], woven(hidden[PAIRS + g][:]), op)

        def quantize_bands(g, held=None, calls=2):
            quantize(g, bands[g][:].rearrange("p b c -> p (b c)"), held, calls)

        output_banks = {}

        def second_layer(lo, hi, at):
            band_codes, band_scales = quantized["w"]
            bank = psum.tile([P, (hi - lo) * GROUP], F32, name=f"output{lo}", tag=f"bank{at}")
            for g in range(lo, hi):
                codes, scales = quantized[g]
                for b in range(2):
                    cols = slice(b * GROUP, (b + 1) * GROUP)
                    nc.tensor.matmul_mx(
                        out=bank[:, (g - lo) * GROUP : (g - lo + 1) * GROUP],
                        lhsT=band_codes[:, cols].bitcast(FP8X4),
                        lhsT_scale=band_scales[:, cols],
                        rhs=codes[:, cols].bitcast(FP8X4),
                        rhs_scale=scales[:, cols],
                        start=(b == 0),
                        stop=(b == 1),
                    )
            output_banks[lo, hi] = bank

        def store(lo, hi, halve):
            result = keep.tile([P, (hi - lo) * GROUP], F32, name=f"result{lo}", align_bytes=256)
            halve(result[:], output_banks[lo, hi][:], 0.5)
            nc.sync.dma_start(out[:, lo * GROUP : hi * GROUP], result[:])

        by_patches(0, 0, 1)
        by_channels(1, 2)
        by_channels(7, 3)
        by_channels(6, 0)
        turn("first0", 4, slots(0))
        haar(1, nc.gpsimd)
        haar_from_psum(0)
        by_patches(2, 1, 2)
        by_channels(8, 3)
        by_patches(9, 0)
        turn("first2", 5, slots(2))
        haar_from_psum(2)
        by_patches(3, 1)
        negated = [keep.tile([P, H // 2], F32, name="negated0", align_bytes=256)]
        nc.vector.tensor_scalar_mul(negated[0][:], hidden[9][:, : H // 2], -1.0)
        quantize_bands(0, 1, 1)
        quantize_bands(1, 2, 1)
        quantize_bands(2, None, 1)
        by_channels(4, 2)
        by_channels(10, 3)
        product_by_channels(5, 0)
        product_by_channels(11, 2)
        negated.append(last.tile([P, H // 2], F32, name="negated1", offset=0, align_bytes=256))
        nc.scalar.mul(negated[1][:], hidden[9][:, H // 2 :], -1.0)
        gelu_by_channels(5)
        gelu_by_channels(11)
        turn("low3", 4, slots(3), slots(9))
        turn("high3", 5, slots(3), lambda t: negated[t // 2][:, (t % 2) * P : (t % 2 + 1) * P])
        second_layer(0, 3, 0)
        haar(4, nc.vector)
        quantize_bands(4)
        second_layer(4, 5, 7)
        haar(5, nc.vector)
        nc.scalar.copy(woven(bands[3][:, 0, :]), turned["low3"])
        nc.scalar.copy(woven(bands[3][:, 1, :]), turned["high3"])
        store(0, 3, nc.scalar.mul)
        store(4, 5, nc.scalar.mul)
        quantize_bands(3)
        second_layer(3, 4, 1)
        store(3, 4, nc.scalar.mul)
        quantize_bands(5)
        second_layer(5, 6, 3)
        store(5, 6, nc.vector.tensor_scalar_mul)
